import numpy as np
import ml_dtypes


def mxq(x, axis, fmt="e4m3"):
    dtype, down = {"e4m3": (ml_dtypes.float8_e4m3fn, 7), "e5m2": (ml_dtypes.float8_e5m2, 14)}[fmt]
    v = np.moveaxis(np.asarray(x, np.float32).astype(ml_dtypes.bfloat16).astype(np.float64), axis, -1)
    blocks = v.reshape(v.shape[:-1] + (-1, 32))
    amax = np.abs(blocks).max(-1, keepdims=True)
    byte = np.maximum(np.where(amax > 0, np.frexp(amax)[1] - 1 + 127, 0) - down, 1)
    scale = np.exp2(byte - 127.0)
    codes = (blocks / scale).astype(np.float32).astype(dtype).astype(np.float64)
    return np.moveaxis((codes * scale).reshape(v.shape), -1, axis)


WIDE = False


def mx_kscale(k):
    if not WIDE:
        return np.ones(k)
    levels = np.array([10, -10, 5, -5, 0])
    if k % 512:
        return np.exp2(np.random.permutation(np.resize(levels, k // 32))).repeat(32)
    a = np.empty((k // 512, 16))
    for p in range(k // 512):
        a[p, :8] = np.random.permutation(np.resize(levels, 8))
        for g in range(8):
            far = levels[np.abs(levels - a[p, g]) >= 10]
            a[p, g + 8] = far[np.random.randint(len(far))]
    return np.exp2(a.ravel()).repeat(32)


def f64(x):
    return np.asarray(x).astype(np.float64)


def striped(idx):
    return np.tile(np.asarray(idx).reshape(-1, 16).T, (8, 1)).astype(np.uint16)


def unstriped(offs):
    return offs[:16].T.reshape(-1).astype(np.int64)


def bf(x):
    return np.asarray(x, np.float32).astype(ml_dtypes.bfloat16)


def planes(Y):
    r, m = Y.shape
    b = f64(bf(Y)).reshape(r // 32, 32, m)
    amax = np.abs(b).max(1)
    byte = np.clip(np.where(amax > 0, np.frexp(amax)[1] - 1 + 127 - 7, 1), 1, 254)
    codes = (b * np.exp2(127.0 - byte)[:, None, :]).reshape(r, m).astype(np.float32).astype(ml_dtypes.float8_e4m3fn).view(np.uint8)
    words = codes.reshape(r // 512, 128, 4, m).transpose(0, 1, 3, 2)
    return np.ascontiguousarray(words), np.ascontiguousarray(byte.astype(np.uint8).reshape(r // 512, 16, m))


E, T, I, J = 512, 1024, 512, 512


def setup_inputs():
    n = np.random.standard_normal
    idx = np.random.permutation(T)[:I]
    idx2 = np.random.permutation(T)[:J]
    fi = mx_kscale(I)
    ti = np.ones(T)
    ti[idx] = fi
    return {
        "first": (n((E, T))).astype(np.float32),
        "second": (n((E, T)) / ti).astype(np.float32),
        "ws": (n((I, J)) * 1 / np.sqrt(I) * fi[:, None]).astype(np.float32),
        "bias": (1.0 * n((J, 1))).astype(np.float32),
        "offs": striped(idx),
        "offs2": striped(idx2),
    }


def reference(first, second, ws, bias, offs, offs2):
    idx = unstriped(offs)
    idx2 = unstriped(offs2)
    vt = f64(second)[:, idx].T
    wsq = mxq(f64(ws), 0, "e4m3")
    vtq = mxq(vt, 0, "e4m3")
    v = wsq.T @ vtq
    ut = f64(first)[:, idx2].T
    y = ut * (v + f64(bias))
    words, scales = planes(y)
    return y, words, scales

@@ -1,0 +1,177 @@
+from contextlib import ExitStack
+
+import concourse.mybir as mybir
+from concourse.masks import make_identity
+
+E, T, I, J = 512, 1024, 512, 512
+FLOPS = 2 * I * J * E
+
+F32 = mybir.dt.float32
+BF16 = mybir.dt.bfloat16
+I32 = mybir.dt.int32
+U32 = mybir.dt.uint32
+U16 = mybir.dt.uint16
+U8 = mybir.dt.uint8
+FP8X4 = mybir.dt.float8_e4m3fn_x4
+ACT = mybir.ActivationFunctionType
+
+P = 128
+PACK = 4
+BLOCKS = E // P
+W_PIECES = 2
+LOAD_ORDER = ("s0", "s1", "s2", "s3", "w0", "w1", "f0", "f1", "f2", "f3")
+ROW = T * 4
+
+
+def tile_attend_spatialgate_pl_kernel(tc, first, second, ws, bias, offs, offs2, out_0, out_1, out_2):
+    nc = tc.nc
+    with ExitStack() as ctx:
+        keep = ctx.enter_context(tc.tile_pool(name="keep", bufs=1))
+        work = ctx.enter_context(tc.tile_pool(name="work", bufs=2))
+        rows = ctx.enter_context(tc.tile_pool(name="rows", bufs=1))
+        psum_t = ctx.enter_context(tc.psum_pool(name="psum_t", bufs=4))
+        psum_v = ctx.enter_context(tc.psum_pool(name="psum_v", bufs=4))
+
+        slots = keep.tile([P, I // 16], U16, name="slots")
+        places = keep.tile([P, J // 16], U16, name="places")
+        bias_cols = keep.tile([P, PACK], F32, name="bias_cols")
+        ident = keep.tile([P, P], F32, name="ident")
+        s_rows = [rows.tile([P, T], F32, name="s_rows%d" % b, offset=b * ROW, align_bytes=64) for b in range(BLOCKS)]
+        f_rows = [
+            rows.tile([P, T], F32, name="f_rows%d" % b, offset=(BLOCKS + b) * ROW, align_bytes=64) for b in range(BLOCKS)
+        ]
+        wj = J // W_PIECES
+        w_raw = [keep.tile([P, PACK, wj], F32, name="w_raw%d" % h) for h in range(W_PIECES)]
+        w_bf = keep.tile([P, PACK, P, PACK], BF16, name="w_bf", align_bytes=64)
+        w_codes = keep.tile([P, J], U32, name="w_codes", align_bytes=64)
+        w_scales = keep.tile([P, J], U8, name="w_scales", align_bytes=64)
+        y_scales = keep.tile([P, E], U8, name="y_scales", align_bytes=64)
+
+        make_identity(nc, ident[:])
+
+        ws_rows = ws.rearrange("(p r) j -> p r j", r=PACK)
+        for n, key in enumerate(LOAD_ORDER):
+            k = int(key[1])
+            if key[0] == "s":
+                nc.sync.dma_start(s_rows[k][:], second[k * P : (k + 1) * P, :])
+            elif key[0] == "f":
+                nc.sync.dma_start(f_rows[k][:], first[k * P : (k + 1) * P, :])
+            else:
+                nc.sync.dma_start(w_raw[k][:], ws_rows[:, :, k * wj : (k + 1) * wj])
+            if n == 0:
+                nc.sync.dma_start(slots[:], offs)
+            if n == 3:
+                nc.sync.dma_start(places[:], offs2)
+                nc.sync.dma_start(bias_cols[:], bias.rearrange("(p t) one -> p (t one)", t=PACK))
+
+        vt_bf = [keep.tile([P, 2 * P * PACK], BF16, name="vt_bf%d" % h, align_bytes=64) for h in range(2)]
+
+        def gather_second(b):
+            picked = work.tile([P, I], BF16, name="picked")
+            nc.vector.tensor_copy(picked[:], s_rows[b][:].indirect(slots[:]))
+            words = picked[:].bitcast(F32)
+            turned = psum_t.tile([P, 2, P], F32, name="turned", tag="turned")
+            for u in range(2):
+                nc.tensor.transpose(turned[:, u, :], words[:, u : I // 2 : 2], ident[:])
+            dst = vt_bf[b // 2][:].bitcast(F32)[:, (b % 2) * 2 * P : (b % 2 + 1) * 2 * P]
+            nc.scalar.copy(dst.rearrange("p (e u) -> p e u", u=2), turned[:].rearrange("p u e -> p e u"))
+
+        def quantize_vt(h):
+            base = (BLOCKS - 1) * ROW + h * 2048
+            codes = rows.tile([P, 2 * P], U32, name="vt_codes%d" % h, offset=base, align_bytes=64)
+            scales = rows.tile([P, 2 * P], U8, name="vt_scales%d" % h, offset=base + 1024, align_bytes=64)
+            nc.vector.quantize_mx(out=codes[:].bitcast(FP8X4), scales=scales[:], in_=vt_bf[h][:])
+            return codes, scales
+
+        def round_ws(h):
+            mw = wj // PACK // 2
+            for half in range(2):
+                m0 = h * wj // PACK + half * mw
+                dst = w_bf[:, :, m0 : m0 + mw, :].rearrange("p t m r -> p m r t")
+                src = w_raw[h][:, :, half * mw * PACK : (half + 1) * mw * PACK].rearrange("p r (m t) -> p m r t", t=PACK)
+                if half == 0:
+                    nc.scalar.copy(dst, src)
+                else:
+                    nc.vector.tensor_copy(dst, src)
+
+        def mix(h, codes, scales):
+            vb = keep.tile([P, PACK, 2 * P], F32, name="vb%d" % h)
+            for pair in range(2):
+                acc = psum_v.tile([P, 2, 2 * P], F32, name="acc")
+                for k in range(2):
+                    cols = slice((2 * pair + k) * P, (2 * pair + k + 1) * P)
+                    nc.tensor.matmul_mx(
+                        out=acc[:, k, :],
+                        lhsT=w_codes[:, cols].bitcast(FP8X4),
+                        lhsT_scale=w_scales[:, cols],
+                        rhs=codes[:].bitcast(FP8X4),
+                        rhs_scale=scales[:],
+                        start=True,
+                        stop=True,
+                    )
+                for k in range(2):
+                    t = 2 * pair + k
+                    nc.scalar.activation(vb[:, t, :], acc[:, k, :], ACT.Identity, bias=bias_cols[:, t : t + 1])
+            return vb
+
+        def gather_first(b):
+            u_cols = work.tile([P, J], F32, name="u_cols")
+            nc.vector.tensor_copy(u_cols[:], f_rows[b][:].indirect(places[:]))
+            ut = psum_t.tile([P, PACK, P], F32, name="ut", tag="turned")
+            for t in range(PACK):
+                nc.tensor.transpose(ut[:, t, :], u_cols[:, t:J:PACK], ident[:])
+            return ut
+
+        out_rows = out_0.rearrange("(p t) e -> p t e", t=PACK)
+        word_rows = out_1.rearrange("z p c r -> p (z c r)").bitcast(I32)
+
+        def gate(b, ut, vb):
+            if b + 1 < BLOCKS:
+                y = rows.tile([P, PACK, P], F32, name="y%d" % b, offset=(BLOCKS + b + 1) * ROW, align_bytes=64)
+            else:
+                y = keep.tile([P, PACK, P], F32, name="y%d" % b)
+            nc.vector.tensor_tensor(y[:], ut[:], vb[:, :, (b % 2) * P : (b % 2 + 1) * P], mybir.AluOpType.mult)
+            nc.sync.dma_start(out_rows[:, :, b * P : (b + 1) * P], y[:])
+            y_bf = work.tile([P, P * PACK], BF16, name="y_bf", align_bytes=64)
+            nc.scalar.copy(
+                y_bf[:].rearrange("p (c i t) -> p c t i", i=4, t=PACK),
+                y[:].rearrange("p t (c i) -> p c t i", i=4),
+            )
+            return y_bf
+
+        def planes(b, y_bf):
+            cols = slice(b * P, (b + 1) * P)
+            if b + 2 < BLOCKS:
+                codes = rows.tile(
+                    [P, P], U32, name="y_codes%d" % b, offset=(BLOCKS + b + 2) * ROW + 2048, align_bytes=64
+                )
+            else:
+                codes = keep.tile([P, P], U32, name="y_codes%d" % b, align_bytes=64)
+            nc.vector.quantize_mx(out=codes[:].bitcast(FP8X4), scales=y_scales[:, cols], in_=y_bf[:])
+            nc.sync.dma_start(word_rows[:, cols], codes[:].bitcast(I32))
+
+        for b in range(BLOCKS):
+            gather_second(b)
+        round_ws(0)
+        q0 = quantize_vt(0)
+        q1 = quantize_vt(1)
+        round_ws(1)
+        nc.vector.quantize_mx(
+            out=w_codes[:].bitcast(FP8X4), scales=w_scales[:], in_=w_bf[:].rearrange("p t m r -> p (t m r)")
+        )
+        vbs = [mix(0, *q0), mix(1, *q1)]
+        uts, ybs = {}, {}
+        for step in range(BLOCKS + 2):
+            if step < BLOCKS:
+                uts[step] = gather_first(step)
+            if 1 <= step <= BLOCKS:
+                ybs[step - 1] = gate(step - 1, uts[step - 1], vbs[(step - 1) // 2])
+            if step >= 2:
+                planes(step - 2, ybs[step - 2])
+
+        scale_rows = out_2.rearrange("z q c -> (z q) c").bitcast(I32)
+        for quad in range(4):
+            queue = nc.sync if quad % 2 == 0 else nc.scalar
+            queue.dma_start(
+                scale_rows[4 * quad : 4 * quad + 4, :], y_scales[32 * quad : 32 * quad + 4, :].bitcast(I32)
+            )

@@ -21,13 +21,13 @@ BLOCKS = E // P
 W_PIECES = 2
 LOAD_ORDER = ("s0", "s1", "s2", "s3", "w0", "w1", "f0", "f1", "f2", "f3")
 ROW = T * 4
+SCALAR_SHARE = 24
 
 
 def tile_attend_spatialgate_pl_kernel(tc, first, second, ws, bias, offs, offs2, out_0, out_1, out_2):
     nc = tc.nc
     with ExitStack() as ctx:
         keep = ctx.enter_context(tc.tile_pool(name="keep", bufs=1))
-        work = ctx.enter_context(tc.tile_pool(name="work", bufs=2))
         rows = ctx.enter_context(tc.tile_pool(name="rows", bufs=1))
         psum_t = ctx.enter_context(tc.psum_pool(name="psum_t", bufs=4))
         psum_v = ctx.enter_context(tc.psum_pool(name="psum_v", bufs=4))
@@ -41,8 +41,11 @@ def tile_attend_spatialgate_pl_kernel(tc, first, second, ws, bias, offs, offs2, 
             rows.tile([P, T], F32, name="f_rows%d" % b, offset=(BLOCKS + b) * ROW, align_bytes=64) for b in range(BLOCKS)
         ]
         wj = J // W_PIECES
-        w_raw = [keep.tile([P, PACK, wj], F32, name="w_raw%d" % h) for h in range(W_PIECES)]
-        w_bf = keep.tile([P, PACK, P, PACK], BF16, name="w_bf", align_bytes=64)
+        w_raw = [
+            rows.tile([P, PACK, wj], F32, name="w_raw%d" % h, offset=(2 * BLOCKS + 1 + h) * ROW, align_bytes=64)
+            for h in range(W_PIECES)
+        ]
+        w_bf = rows.tile([P, PACK, P, PACK], BF16, name="w_bf", offset=2 * BLOCKS * ROW, align_bytes=64)
         w_codes = keep.tile([P, J], U32, name="w_codes", align_bytes=64)
         w_scales = keep.tile([P, J], U8, name="w_scales", align_bytes=64)
         y_scales = keep.tile([P, E], U8, name="y_scales", align_bytes=64)
@@ -67,7 +70,10 @@ def tile_attend_spatialgate_pl_kernel(tc, first, second, ws, bias, offs, offs2, 
         vt_bf = [keep.tile([P, 2 * P * PACK], BF16, name="vt_bf%d" % h, align_bytes=64) for h in range(2)]
 
         def gather_second(b):
-            picked = work.tile([P, I], BF16, name="picked")
+            if b == BLOCKS - 2:
+                picked = rows.tile([P, I], BF16, name="picked_last", offset=2 * BLOCKS * ROW, align_bytes=64)
+            else:
+                picked = keep.tile([P, I], BF16, name="picked%d" % b)
             nc.vector.tensor_copy(picked[:], s_rows[b][:].indirect(slots[:]))
             words = picked[:].bitcast(F32)
             turned = psum_t.tile([P, 2, P], F32, name="turned", tag="turned")
@@ -77,22 +83,18 @@ def tile_attend_spatialgate_pl_kernel(tc, first, second, ws, bias, offs, offs2, 
             nc.scalar.copy(dst.rearrange("p (e u) -> p e u", u=2), turned[:].rearrange("p u e -> p e u"))
 
         def quantize_vt(h):
-            base = (BLOCKS - 1) * ROW + h * 2048
+            base = (BLOCKS - 2) * ROW + h * 2048
             codes = rows.tile([P, 2 * P], U32, name="vt_codes%d" % h, offset=base, align_bytes=64)
             scales = rows.tile([P, 2 * P], U8, name="vt_scales%d" % h, offset=base + 1024, align_bytes=64)
             nc.vector.quantize_mx(out=codes[:].bitcast(FP8X4), scales=scales[:], in_=vt_bf[h][:])
             return codes, scales
 
         def round_ws(h):
-            mw = wj // PACK // 2
-            for half in range(2):
-                m0 = h * wj // PACK + half * mw
-                dst = w_bf[:, :, m0 : m0 + mw, :].rearrange("p t m r -> p m r t")
-                src = w_raw[h][:, :, half * mw * PACK : (half + 1) * mw * PACK].rearrange("p r (m t) -> p m r t", t=PACK)
-                if half == 0:
-                    nc.scalar.copy(dst, src)
-                else:
-                    nc.vector.tensor_copy(dst, src)
+            mw = wj // PACK
+            for copy, m_from, m_to in ((nc.scalar.copy, 0, SCALAR_SHARE), (nc.vector.tensor_copy, SCALAR_SHARE, mw)):
+                dst = w_bf[:, :, h * mw + m_from : h * mw + m_to, :].rearrange("p t m r -> p m r t")
+                src = w_raw[h][:, :, m_from * PACK : m_to * PACK].rearrange("p r (m t) -> p m r t", t=PACK)
+                copy(dst, src)
 
         def mix(h, codes, scales):
             vb = keep.tile([P, PACK, 2 * P], F32, name="vb%d" % h)
@@ -115,7 +117,8 @@ def tile_attend_spatialgate_pl_kernel(tc, first, second, ws, bias, offs, offs2, 
             return vb
 
         def gather_first(b):
-            u_cols = work.tile([P, J], F32, name="u_cols")
+            u_offset = (2 * BLOCKS + 2) * ROW + b * 2048 if b < 2 else (BLOCKS + b - 2) * ROW
+            u_cols = rows.tile([P, J], F32, name="u_cols%d" % b, offset=u_offset, align_bytes=64)
             nc.vector.tensor_copy(u_cols[:], f_rows[b][:].indirect(places[:]))
             ut = psum_t.tile([P, PACK, P], F32, name="ut", tag="turned")
             for t in range(PACK):
@@ -125,49 +128,52 @@ def tile_attend_spatialgate_pl_kernel(tc, first, second, ws, bias, offs, offs2, 
         out_rows = out_0.rearrange("(p t) e -> p t e", t=PACK)
         word_rows = out_1.rearrange("z p c r -> p (z c r)").bitcast(I32)
 
-        def gate(b, ut, vb):
-            if b + 1 < BLOCKS:
-                y = rows.tile([P, PACK, P], F32, name="y%d" % b, offset=(BLOCKS + b + 1) * ROW, align_bytes=64)
+        y_offset = {0: (BLOCKS + 1) * ROW + 2048, 1: (BLOCKS + 3) * ROW, 2: (BLOCKS + 3) * ROW + 2048}
+        y_bf = keep.tile([P, E * PACK], BF16, name="y_bf", align_bytes=64)
+        y_codes = keep.tile([P, E], U32, name="y_codes", align_bytes=64)
+
+        def gate(b, ut, vb, parts):
+            if b in y_offset:
+                y = rows.tile([P, PACK, P], F32, name="y%d" % b, offset=y_offset[b], align_bytes=64)
             else:
                 y = keep.tile([P, PACK, P], F32, name="y%d" % b)
-            nc.vector.tensor_tensor(y[:], ut[:], vb[:, :, (b % 2) * P : (b % 2 + 1) * P], mybir.AluOpType.mult)
-            nc.sync.dma_start(out_rows[:, :, b * P : (b + 1) * P], y[:])
-            y_bf = work.tile([P, P * PACK], BF16, name="y_bf", align_bytes=64)
-            nc.scalar.copy(
-                y_bf[:].rearrange("p (c i t) -> p c t i", i=4, t=PACK),
-                y[:].rearrange("p t (c i) -> p c t i", i=4),
-            )
-            return y_bf
-
-        def planes(b, y_bf):
-            cols = slice(b * P, (b + 1) * P)
-            if b + 2 < BLOCKS:
-                codes = rows.tile(
-                    [P, P], U32, name="y_codes%d" % b, offset=(BLOCKS + b + 2) * ROW + 2048, align_bytes=64
+            width = P // parts
+            for part in range(parts):
+                cols = slice(part * width, (part + 1) * width)
+                e0 = (b % 2) * P + part * width
+                nc.vector.tensor_tensor(y[:, :, cols], ut[:, :, cols], vb[:, :, e0 : e0 + width], mybir.AluOpType.mult)
+                c0 = (b * P + part * width) * PACK
+                nc.scalar.copy(
+                    y_bf[:, c0 : c0 + width * PACK].rearrange("p (c i t) -> p c t i", i=4, t=PACK),
+                    y[:, :, cols].rearrange("p t (c i) -> p c t i", i=4),
                 )
-            else:
-                codes = keep.tile([P, P], U32, name="y_codes%d" % b, align_bytes=64)
-            nc.vector.quantize_mx(out=codes[:].bitcast(FP8X4), scales=y_scales[:, cols], in_=y_bf[:])
-            nc.sync.dma_start(word_rows[:, cols], codes[:].bitcast(I32))
+            nc.sync.dma_start(out_rows[:, :, b * P : (b + 1) * P], y[:])
+
+        def planes(e_from, e_to):
+            cols = slice(e_from, e_to)
+            nc.vector.quantize_mx(
+                out=y_codes[:, cols].bitcast(FP8X4), scales=y_scales[:, cols], in_=y_bf[:, e_from * PACK : e_to * PACK]
+            )
+            nc.sync.dma_start(word_rows[:, cols], y_codes[:, cols].bitcast(I32))
 
         for b in range(BLOCKS):
             gather_second(b)
-        round_ws(0)
         q0 = quantize_vt(0)
+        round_ws(0)
         q1 = quantize_vt(1)
         round_ws(1)
         nc.vector.quantize_mx(
             out=w_codes[:].bitcast(FP8X4), scales=w_scales[:], in_=w_bf[:].rearrange("p t m r -> p (t m r)")
         )
         vbs = [mix(0, *q0), mix(1, *q1)]
-        uts, ybs = {}, {}
-        for step in range(BLOCKS + 2):
-            if step < BLOCKS:
-                uts[step] = gather_first(step)
-            if 1 <= step <= BLOCKS:
-                ybs[step - 1] = gate(step - 1, uts[step - 1], vbs[(step - 1) // 2])
-            if step >= 2:
-                planes(step - 2, ybs[step - 2])
+        uts = [gather_first(b) for b in range(BLOCKS - 1)]
+        gate(0, uts[0], vbs[0], 1)
+        uts.append(gather_first(BLOCKS - 1))
+        gate(1, uts[1], vbs[0], 1)
+        gate(2, uts[2], vbs[1], 1)
+        planes(0, 2 * P)
+        gate(3, uts[3], vbs[1], 2)
+        planes(2 * P, 4 * P)
 
         scale_rows = out_2.rearrange("z q c -> (z q) c").bitcast(I32)
         for quad in range(4):

@@ -128,7 +128,7 @@ def tile_attend_spatialgate_pl_kernel(tc, first, second, ws, bias, offs, offs2, 
         out_rows = out_0.rearrange("(p t) e -> p t e", t=PACK)
         word_rows = out_1.rearrange("z p c r -> p (z c r)").bitcast(I32)
 
-        y_offset = {0: (BLOCKS + 1) * ROW + 2048, 1: (BLOCKS + 3) * ROW, 2: (BLOCKS + 3) * ROW + 2048}
+        y_offset = {1: (BLOCKS + 3) * ROW, 2: (BLOCKS + 3) * ROW + 2048}
         y_bf = keep.tile([P, E * PACK], BF16, name="y_bf", align_bytes=64)
         y_codes = keep.tile([P, E], U32, name="y_codes", align_bytes=64)
 
@@ -141,7 +141,14 @@ def tile_attend_spatialgate_pl_kernel(tc, first, second, ws, bias, offs, offs2, 
             for part in range(parts):
                 cols = slice(part * width, (part + 1) * width)
                 e0 = (b % 2) * P + part * width
-                nc.vector.tensor_tensor(y[:, :, cols], ut[:, :, cols], vb[:, :, e0 : e0 + width], mybir.AluOpType.mult)
+                if b == 0:
+                    ut_sb = keep.tile([P, PACK, P], F32, name="ut_sb")
+                    nc.scalar.copy(ut_sb[:], ut[:])
+                    nc.gpsimd.tensor_tensor(y[:], ut_sb[:], vb[:, :, e0 : e0 + width], mybir.AluOpType.mult)
+                else:
+                    nc.vector.tensor_tensor(
+                        y[:, :, cols], ut[:, :, cols], vb[:, :, e0 : e0 + width], mybir.AluOpType.mult
+                    )
                 c0 = (b * P + part * width) * PACK
                 nc.scalar.copy(
                     y_bf[:, c0 : c0 + width * PACK].rearrange("p (c i t) -> p c t i", i=4, t=PACK),
@@ -165,10 +172,11 @@ def tile_attend_spatialgate_pl_kernel(tc, first, second, ws, bias, offs, offs2, 
         nc.vector.quantize_mx(
             out=w_codes[:].bitcast(FP8X4), scales=w_scales[:], in_=w_bf[:].rearrange("p t m r -> p (t m r)")
         )
-        vbs = [mix(0, *q0), mix(1, *q1)]
-        uts = [gather_first(b) for b in range(BLOCKS - 1)]
+        vbs = [mix(0, *q0)]
+        uts = [gather_first(0)]
         gate(0, uts[0], vbs[0], 1)
-        uts.append(gather_first(BLOCKS - 1))
+        vbs.append(mix(1, *q1))
+        uts.extend(gather_first(b) for b in range(1, BLOCKS))
         gate(1, uts[1], vbs[0], 1)
         gate(2, uts[2], vbs[1], 1)
         planes(0, 2 * P)

@@ -21,7 +21,7 @@ BLOCKS = E // P
 W_PIECES = 2
 LOAD_ORDER = ("s0", "s1", "s2", "s3", "w0", "w1", "f0", "f1", "f2", "f3")
 ROW = T * 4
-SCALAR_SHARE = 24
+SCALAR_SHARE = (24, 24)
 
 
 def tile_attend_spatialgate_pl_kernel(tc, first, second, ws, bias, offs, offs2, out_0, out_1, out_2):
@@ -91,7 +91,7 @@ def tile_attend_spatialgate_pl_kernel(tc, first, second, ws, bias, offs, offs2, 
 
         def round_ws(h):
             mw = wj // PACK
-            for copy, m_from, m_to in ((nc.scalar.copy, 0, SCALAR_SHARE), (nc.vector.tensor_copy, SCALAR_SHARE, mw)):
+            for copy, m_from, m_to in ((nc.scalar.copy, 0, SCALAR_SHARE[h]), (nc.vector.tensor_copy, SCALAR_SHARE[h], mw)):
                 dst = w_bf[:, :, h * mw + m_from : h * mw + m_to, :].rearrange("p t m r -> p m r t")
                 src = w_raw[h][:, :, m_from * PACK : m_to * PACK].rearrange("p r (m t) -> p m r t", t=PACK)
                 copy(dst, src)
@@ -128,7 +128,7 @@ def tile_attend_spatialgate_pl_kernel(tc, first, second, ws, bias, offs, offs2, 
         out_rows = out_0.rearrange("(p t) e -> p t e", t=PACK)
         word_rows = out_1.rearrange("z p c r -> p (z c r)").bitcast(I32)
 
-        y_offset = {1: (BLOCKS + 3) * ROW, 2: (BLOCKS + 3) * ROW + 2048}
+        y_offset = {1: BLOCKS * ROW - 1024, 2: BLOCKS * ROW + 1024}
         y_bf = keep.tile([P, E * PACK], BF16, name="y_bf", align_bytes=64)
         y_codes = keep.tile([P, E], U32, name="y_codes", align_bytes=64)
 
@@ -161,7 +161,9 @@ def tile_attend_spatialgate_pl_kernel(tc, first, second, ws, bias, offs, offs2, 
             nc.vector.quantize_mx(
                 out=y_codes[:, cols].bitcast(FP8X4), scales=y_scales[:, cols], in_=y_bf[:, e_from * PACK : e_to * PACK]
             )
-            nc.sync.dma_start(word_rows[:, cols], y_codes[:, cols].bitcast(I32))
+
+        def store_words(e_from, e_to):
+            nc.sync.dma_start(word_rows[:, e_from:e_to], y_codes[:, e_from:e_to].bitcast(I32))
 
         for b in range(BLOCKS):
             gather_second(b)
@@ -180,8 +182,11 @@ def tile_attend_spatialgate_pl_kernel(tc, first, second, ws, bias, offs, offs2, 
         gate(1, uts[1], vbs[0], 1)
         gate(2, uts[2], vbs[1], 1)
         planes(0, 2 * P)
+        store_words(0, 2 * P)
         gate(3, uts[3], vbs[1], 2)
-        planes(2 * P, 4 * P)
+        planes(2 * P, 3 * P)
+        planes(3 * P, 4 * P)
+        store_words(2 * P, 4 * P)
 
         scale_rows = out_2.rearrange("z q c -> (z q) c").bitcast(I32)
         for quad in range(4):

@@ -14,14 +14,18 @@ U16 = mybir.dt.uint16
 U8 = mybir.dt.uint8
 FP8X4 = mybir.dt.float8_e4m3fn_x4
 ACT = mybir.ActivationFunctionType
+ALU = mybir.AluOpType
 
 P = 128
 PACK = 4
 BLOCKS = E // P
 W_PIECES = 2
-LOAD_ORDER = ("s0", "s1", "s2", "s3", "w0", "w1", "f0", "f1", "f2", "f3")
 ROW = T * 4
-SCALAR_SHARE = (24, 24)
+BANK = 2048
+W_SCALAR = (32, 24)
+S_SCALAR = (0, 0, 20, 16)
+F_SCALAR = (12, 20, 20, 32)
+KB = 1024
 
 
 def tile_attend_spatialgate_pl_kernel(tc, first, second, ws, bias, offs, offs2, out_0, out_1, out_2):
@@ -29,81 +33,106 @@ def tile_attend_spatialgate_pl_kernel(tc, first, second, ws, bias, offs, offs2, 
     with ExitStack() as ctx:
         keep = ctx.enter_context(tc.tile_pool(name="keep", bufs=1))
         rows = ctx.enter_context(tc.tile_pool(name="rows", bufs=1))
-        psum_t = ctx.enter_context(tc.psum_pool(name="psum_t", bufs=4))
-        psum_v = ctx.enter_context(tc.psum_pool(name="psum_v", bufs=4))
+        psum = ctx.enter_context(tc.psum_pool(name="psum", bufs=1))
 
         slots = keep.tile([P, I // 16], U16, name="slots")
         places = keep.tile([P, J // 16], U16, name="places")
         bias_cols = keep.tile([P, PACK], F32, name="bias_cols")
         ident = keep.tile([P, P], F32, name="ident")
-        s_rows = [rows.tile([P, T], F32, name="s_rows%d" % b, offset=b * ROW, align_bytes=64) for b in range(BLOCKS)]
-        f_rows = [
-            rows.tile([P, T], F32, name="f_rows%d" % b, offset=(BLOCKS + b) * ROW, align_bytes=64) for b in range(BLOCKS)
-        ]
         wj = J // W_PIECES
         w_raw = [
-            rows.tile([P, PACK, wj], F32, name="w_raw%d" % h, offset=(2 * BLOCKS + 1 + h) * ROW, align_bytes=64)
-            for h in range(W_PIECES)
+            keep.tile([P, PACK, wj], F32, name="w_raw0"),
+            rows.tile([P, PACK, wj], F32, name="w_raw1", offset=24 * KB, align_bytes=64),
         ]
-        w_bf = rows.tile([P, PACK, P, PACK], BF16, name="w_bf", offset=2 * BLOCKS * ROW, align_bytes=64)
+        w_bf = rows.tile([P, PACK, P, PACK], BF16, name="w_bf", offset=32 * KB, align_bytes=64)
         w_codes = keep.tile([P, J], U32, name="w_codes", align_bytes=64)
         w_scales = keep.tile([P, J], U8, name="w_scales", align_bytes=64)
+        y_bf = keep.tile([P, E * PACK], BF16, name="y_bf", align_bytes=64)
+        y_codes = rows.tile([P, E], U32, name="y_codes", offset=3 * ROW, align_bytes=64)
         y_scales = keep.tile([P, E], U8, name="y_scales", align_bytes=64)
+        s_rows = [keep.tile([P, T], F32, name="s_rows%d" % b) for b in range(BLOCKS)]
+        f_rows = [rows.tile([P, T], F32, name="f_rows%d" % b, offset=b * ROW, align_bytes=64) for b in range(BLOCKS)]
+        picked_at = (32 * KB, 36 * KB, 24 * KB, 27 * KB)
+        vt_at = (40 * KB, 41 * KB, 42 * KB, 45 * KB)
+        codes_at = {0: 46 * KB, 2: 48 * KB, 3: 51 * KB}
+        u_at = (24 * KB + 512, vt_at[2], codes_at[2], 25 * KB + 512)
+        vb_at = {0: 20 * KB + 512, 2: 52 * KB, 3: 3 * ROW + 2 * KB}
+        turned_bank = (0, 1, 0, 1)
+        acc_bank = {0: 2, 2: 0, 3: 1}
+        ut_bank = (4, 5, 6, 7)
+        vt_pair = rows.tile([P, 2 * P * PACK], BF16, name="vt_pair", offset=vt_at[0], align_bytes=64)
 
         make_identity(nc, ident[:])
 
         ws_rows = ws.rearrange("(p r) j -> p r j", r=PACK)
-        for n, key in enumerate(LOAD_ORDER):
-            k = int(key[1])
-            if key[0] == "s":
-                nc.sync.dma_start(s_rows[k][:], second[k * P : (k + 1) * P, :])
-            elif key[0] == "f":
-                nc.sync.dma_start(f_rows[k][:], first[k * P : (k + 1) * P, :])
-            else:
-                nc.sync.dma_start(w_raw[k][:], ws_rows[:, :, k * wj : (k + 1) * wj])
-            if n == 0:
-                nc.sync.dma_start(slots[:], offs)
-            if n == 3:
-                nc.sync.dma_start(places[:], offs2)
-                nc.sync.dma_start(bias_cols[:], bias.rearrange("(p t) one -> p (t one)", t=PACK))
 
-        vt_bf = [keep.tile([P, 2 * P * PACK], BF16, name="vt_bf%d" % h, align_bytes=64) for h in range(2)]
+        def load_w(h):
+            nc.sync.dma_start(w_raw[h][:], ws_rows[:, :, h * wj : (h + 1) * wj])
 
-        def gather_second(b):
-            if b == BLOCKS - 2:
-                picked = rows.tile([P, I], BF16, name="picked_last", offset=2 * BLOCKS * ROW, align_bytes=64)
-            else:
-                picked = keep.tile([P, I], BF16, name="picked%d" % b)
-            nc.vector.tensor_copy(picked[:], s_rows[b][:].indirect(slots[:]))
-            words = picked[:].bitcast(F32)
-            turned = psum_t.tile([P, 2, P], F32, name="turned", tag="turned")
-            for u in range(2):
-                nc.tensor.transpose(turned[:, u, :], words[:, u : I // 2 : 2], ident[:])
-            dst = vt_bf[b // 2][:].bitcast(F32)[:, (b % 2) * 2 * P : (b % 2 + 1) * 2 * P]
-            nc.scalar.copy(dst.rearrange("p (e u) -> p e u", u=2), turned[:].rearrange("p u e -> p e u"))
+        def load_s(b):
+            nc.sync.dma_start(s_rows[b][:], second[b * P : (b + 1) * P, :])
 
-        def quantize_vt(h):
-            base = (BLOCKS - 2) * ROW + h * 2048
-            codes = rows.tile([P, 2 * P], U32, name="vt_codes%d" % h, offset=base, align_bytes=64)
-            scales = rows.tile([P, 2 * P], U8, name="vt_scales%d" % h, offset=base + 1024, align_bytes=64)
-            nc.vector.quantize_mx(out=codes[:].bitcast(FP8X4), scales=scales[:], in_=vt_bf[h][:])
-            return codes, scales
+        def load_f(b):
+            nc.sync.dma_start(f_rows[b][:], first[b * P : (b + 1) * P, :])
+
+        load_s(0)
+        nc.sync.dma_start(slots[:], offs)
+        load_s(1)
+        load_w(0)
+        load_w(1)
+        load_s(2)
+        load_s(3)
+        nc.sync.dma_start(bias_cols[:], bias.rearrange("(p t) one -> p (t one)", t=PACK))
+        nc.sync.dma_start(places[:], offs2)
+        for b in range(BLOCKS):
+            load_f(b)
 
         def round_ws(h):
             mw = wj // PACK
-            for copy, m_from, m_to in ((nc.scalar.copy, 0, SCALAR_SHARE[h]), (nc.vector.tensor_copy, SCALAR_SHARE[h], mw)):
+            for copy, m_from, m_to in ((nc.scalar.copy, 0, W_SCALAR[h]), (nc.vector.tensor_copy, W_SCALAR[h], mw)):
                 dst = w_bf[:, :, h * mw + m_from : h * mw + m_to, :].rearrange("p t m r -> p m r t")
                 src = w_raw[h][:, :, m_from * PACK : m_to * PACK].rearrange("p r (m t) -> p m r t", t=PACK)
                 copy(dst, src)
 
-        def mix(h, codes, scales):
-            vb = keep.tile([P, PACK, 2 * P], F32, name="vb%d" % h)
-            for pair in range(2):
-                acc = psum_v.tile([P, 2, 2 * P], F32, name="acc")
-                for k in range(2):
-                    cols = slice((2 * pair + k) * P, (2 * pair + k + 1) * P)
+        def gather_second(b):
+            picked = rows.tile([P, I], BF16, name="picked%d" % b, offset=picked_at[b], align_bytes=64)
+            cut = S_SCALAR[b]
+            if cut > 0:
+                nc.scalar.activation(picked[:, : cut * 16], s_rows[b][:].indirect(slots[:, :cut]), ACT.Copy)
+            if cut < I // 16:
+                nc.vector.tensor_copy(picked[:, cut * 16 :], s_rows[b][:].indirect(slots[:, cut:]))
+            words = picked[:].bitcast(F32)
+            turned = psum.tile([P, 2, P], F32, name="turned%d" % b, offset=turned_bank[b] * BANK)
+            for u in range(2):
+                nc.tensor.transpose(turned[:, u, :], words[:, u : I // 2 : 2], ident[:])
+            return turned
+
+        def copy_turned(b, turned):
+            if b < 2:
+                vt_bf = vt_pair[:, b * P * PACK : (b + 1) * P * PACK]
+            else:
+                vt_tile = rows.tile([P, P * PACK], BF16, name="vt_bf%d" % b, offset=vt_at[b], align_bytes=64)
+                vt_bf = vt_tile[:]
+            nc.scalar.copy(vt_bf.bitcast(F32).rearrange("p (e u) -> p e u", u=2), turned[:].rearrange("p u e -> p e u"))
+            return vt_bf
+
+        def quantize_vt(b, vt_bf, n):
+            codes = rows.tile([P, n], U32, name="vt_codes%d" % b, offset=codes_at[b], align_bytes=64)
+            scales = keep.tile([P, n], U8, name="vt_scales%d" % b, align_bytes=64)
+            nc.vector.quantize_mx(out=codes[:].bitcast(FP8X4), scales=scales[:], in_=vt_bf)
+            return codes, scales
+
+        def mix(b, codes, scales, n):
+            per_bank = BANK // (4 * n)
+            banks = []
+            for k in range(PACK // per_bank):
+                acc = psum.tile([P, per_bank, n], F32, name="acc%d_%d" % (b, k), offset=(acc_bank[b] + k) * BANK)
+                banks.append(acc)
+                for s in range(per_bank):
+                    t = k * per_bank + s
+                    cols = slice(t * P, (t + 1) * P)
                     nc.tensor.matmul_mx(
-                        out=acc[:, k, :],
+                        out=acc[:, s, :],
                         lhsT=w_codes[:, cols].bitcast(FP8X4),
                         lhsT_scale=w_scales[:, cols],
                         rhs=codes[:].bitcast(FP8X4),
@@ -111,82 +140,111 @@ def tile_attend_spatialgate_pl_kernel(tc, first, second, ws, bias, offs, offs2, 
                         start=True,
                         stop=True,
                     )
-                for k in range(2):
-                    t = 2 * pair + k
-                    nc.scalar.activation(vb[:, t, :], acc[:, k, :], ACT.Identity, bias=bias_cols[:, t : t + 1])
-            return vb
+            return banks
+
+        def add_bias(vb, acc, t_from, on_vector):
+            count, n = acc.shape[1], acc.shape[2]
+            if on_vector:
+                spread = bias_cols[:, t_from : t_from + count].unsqueeze(2).to_broadcast([P, count, n])
+                nc.vector.tensor_tensor(vb[:, t_from : t_from + count, :], acc[:], spread, ALU.add)
+            else:
+                for s in range(count):
+                    t = t_from + s
+                    nc.scalar.activation(vb[:, t, :], acc[:, s, :], ACT.Identity, bias=bias_cols[:, t : t + 1])
+
+        def vb_tile(b, n):
+            return rows.tile([P, PACK, n], F32, name="vb%d" % b, offset=vb_at[b], align_bytes=64)
 
         def gather_first(b):
-            u_offset = (2 * BLOCKS + 2) * ROW + b * 2048 if b < 2 else (BLOCKS + b - 2) * ROW
-            u_cols = rows.tile([P, J], F32, name="u_cols%d" % b, offset=u_offset, align_bytes=64)
-            nc.vector.tensor_copy(u_cols[:], f_rows[b][:].indirect(places[:]))
-            ut = psum_t.tile([P, PACK, P], F32, name="ut", tag="turned")
+            u_cols = rows.tile([P, J], F32, name="u_cols%d" % b, offset=u_at[b], align_bytes=64)
+            cut = F_SCALAR[b]
+            nc.scalar.activation(u_cols[:, : cut * 16], f_rows[b][:].indirect(places[:, :cut]), ACT.Copy)
+            if cut < J // 16:
+                nc.vector.tensor_copy(u_cols[:, cut * 16 :], f_rows[b][:].indirect(places[:, cut:]))
+            ut = psum.tile([P, PACK, P], F32, name="ut%d" % b, offset=ut_bank[b] * BANK)
             for t in range(PACK):
                 nc.tensor.transpose(ut[:, t, :], u_cols[:, t:J:PACK], ident[:])
             return ut
 
+        ys = [keep.tile([P, PACK, P], F32, name="y%d" % b) for b in range(BLOCKS)]
         out_rows = out_0.rearrange("(p t) e -> p t e", t=PACK)
         word_rows = out_1.rearrange("z p c r -> p (z c r)").bitcast(I32)
 
-        y_offset = {1: BLOCKS * ROW - 1024, 2: BLOCKS * ROW + 1024}
-        y_bf = keep.tile([P, E * PACK], BF16, name="y_bf", align_bytes=64)
-        y_codes = keep.tile([P, E], U32, name="y_codes", align_bytes=64)
+        def gate(b, ut, vb, cols):
+            nc.vector.tensor_tensor(ys[b][:, :, cols], ut[:, :, cols], vb[:, :, cols], ALU.mult)
 
-        def gate(b, ut, vb, parts):
-            if b in y_offset:
-                y = rows.tile([P, PACK, P], F32, name="y%d" % b, offset=y_offset[b], align_bytes=64)
+        def round_y(b, cols, engine):
+            c0 = (b * P + cols.start) * PACK
+            dst = y_bf[:, c0 : c0 + (cols.stop - cols.start) * PACK].rearrange("p (c i t) -> p c t i", i=4, t=PACK)
+            src = ys[b][:, :, cols].rearrange("p t (c i) -> p c t i", i=4)
+            if engine == "gpsimd":
+                nc.gpsimd.tensor_scalar(dst, src, 1.0, -0.0, ALU.mult, ALU.add)
+            elif engine == "vector":
+                nc.vector.tensor_copy(dst, src)
             else:
-                y = keep.tile([P, PACK, P], F32, name="y%d" % b)
-            width = P // parts
-            for part in range(parts):
-                cols = slice(part * width, (part + 1) * width)
-                e0 = (b % 2) * P + part * width
-                if b == 0:
-                    ut_sb = keep.tile([P, PACK, P], F32, name="ut_sb")
-                    nc.scalar.copy(ut_sb[:], ut[:])
-                    nc.gpsimd.tensor_tensor(y[:], ut_sb[:], vb[:, :, e0 : e0 + width], mybir.AluOpType.mult)
-                else:
-                    nc.vector.tensor_tensor(
-                        y[:, :, cols], ut[:, :, cols], vb[:, :, e0 : e0 + width], mybir.AluOpType.mult
-                    )
-                c0 = (b * P + part * width) * PACK
-                nc.scalar.copy(
-                    y_bf[:, c0 : c0 + width * PACK].rearrange("p (c i t) -> p c t i", i=4, t=PACK),
-                    y[:, :, cols].rearrange("p t (c i) -> p c t i", i=4),
-                )
-            nc.sync.dma_start(out_rows[:, :, b * P : (b + 1) * P], y[:])
+                nc.scalar.copy(dst, src)
 
-        def planes(e_from, e_to):
-            cols = slice(e_from, e_to)
+        def store_y(b):
+            nc.sync.dma_start(out_rows[:, :, b * P : (b + 1) * P], ys[b][:])
+
+        def planes(b_from, b_to):
+            cols = slice(b_from * P, b_to * P)
             nc.vector.quantize_mx(
-                out=y_codes[:, cols].bitcast(FP8X4), scales=y_scales[:, cols], in_=y_bf[:, e_from * PACK : e_to * PACK]
+                out=y_codes[:, cols].bitcast(FP8X4),
+                scales=y_scales[:, cols],
+                in_=y_bf[:, b_from * P * PACK : b_to * P * PACK],
             )
 
         def store_words(e_from, e_to):
             nc.sync.dma_start(word_rows[:, e_from:e_to], y_codes[:, e_from:e_to].bitcast(I32))
 
-        for b in range(BLOCKS):
-            gather_second(b)
-        q0 = quantize_vt(0)
+        t0 = gather_second(0)
+        t1 = gather_second(1)
+        copy_turned(0, t0)
         round_ws(0)
-        q1 = quantize_vt(1)
+        copy_turned(1, t1)
         round_ws(1)
+        q01 = quantize_vt(0, vt_pair[:], 2 * P)
         nc.vector.quantize_mx(
             out=w_codes[:].bitcast(FP8X4), scales=w_scales[:], in_=w_bf[:].rearrange("p t m r -> p (t m r)")
         )
-        vbs = [mix(0, *q0)]
-        uts = [gather_first(0)]
-        gate(0, uts[0], vbs[0], 1)
-        vbs.append(mix(1, *q1))
-        uts.extend(gather_first(b) for b in range(1, BLOCKS))
-        gate(1, uts[1], vbs[0], 1)
-        gate(2, uts[2], vbs[1], 1)
-        planes(0, 2 * P)
-        store_words(0, 2 * P)
-        gate(3, uts[3], vbs[1], 2)
-        planes(2 * P, 3 * P)
-        planes(3 * P, 4 * P)
-        store_words(2 * P, 4 * P)
+        a01 = mix(0, *q01, 2 * P)
+        t2 = gather_second(2)
+        t3 = gather_second(3)
+        vt2 = copy_turned(2, t2)
+        vb01 = vb_tile(0, 2 * P)
+        add_bias(vb01, a01[0], 0, True)
+        add_bias(vb01, a01[1], 2, False)
+        a2 = mix(2, *quantize_vt(2, vt2, P), P)
+        vt3 = copy_turned(3, t3)
+        u0 = gather_first(0)
+        a3 = mix(3, *quantize_vt(3, vt3, P), P)
+        u1 = gather_first(1)
+        vb2 = vb_tile(2, P)
+        add_bias(vb2, a2[0], 0, True)
+        u2 = gather_first(2)
+        whole = slice(0, P)
+        halves = (slice(0, P // 2), slice(P // 2, P))
+        gate(0, u0, vb01[:, :, :P], whole)
+        store_y(0)
+        round_y(0, whole, "gpsimd")
+        u3 = gather_first(3)
+        vb3 = vb_tile(3, P)
+        add_bias(vb3, a3[0], 0, False)
+        gate(1, u1, vb01[:, :, P:], whole)
+        store_y(1)
+        gate(2, u2, vb2, whole)
+        store_y(2)
+        round_y(1, whole, "vector")
+        round_y(2, whole, "scalar")
+        for cols in halves:
+            gate(3, u3, vb3, cols)
+            round_y(3, cols, "scalar")
+        store_y(3)
+        planes(0, 3)
+        store_words(0, 3 * P)
+        planes(3, 4)
+        store_words(3 * P, 4 * P)
 
         scale_rows = out_2.rearrange("z q c -> (z q) c").bitcast(I32)
         for quad in range(4):

@@ -22,9 +22,9 @@ BLOCKS = E // P
 W_PIECES = 2
 ROW = T * 4
 BANK = 2048
-W_SCALAR = (32, 24)
-S_SCALAR = (0, 0, 20, 16)
-F_SCALAR = (12, 20, 20, 32)
+W_SCALAR = (32, 12)
+S_SCALAR = (0, 0, 26, 16)
+F_SCALAR = (0, 32, 0, 24)
 KB = 1024
 
 
@@ -52,11 +52,11 @@ def tile_attend_spatialgate_pl_kernel(tc, first, second, ws, bias, offs, offs2, 
         y_scales = keep.tile([P, E], U8, name="y_scales", align_bytes=64)
         s_rows = [keep.tile([P, T], F32, name="s_rows%d" % b) for b in range(BLOCKS)]
         f_rows = [rows.tile([P, T], F32, name="f_rows%d" % b, offset=b * ROW, align_bytes=64) for b in range(BLOCKS)]
-        picked_at = (32 * KB, 36 * KB, 24 * KB, 27 * KB)
+        picked_at = (32 * KB, 36 * KB, 24 * KB, 35 * KB)
         vt_at = (40 * KB, 41 * KB, 42 * KB, 45 * KB)
-        codes_at = {0: 46 * KB, 2: 48 * KB, 3: 51 * KB}
-        u_at = (24 * KB + 512, vt_at[2], codes_at[2], 25 * KB + 512)
-        vb_at = {0: 20 * KB + 512, 2: 52 * KB, 3: 3 * ROW + 2 * KB}
+        codes_at = {0: 47 * KB, 2: 48 * KB, 3: 51 * KB}
+        u_at = (vt_at[2], picked_at[3], vt_at[3], vt_at[2])
+        vb_at = {0: 16 * KB, 2: 52 * KB, 3: 3 * ROW + 2 * KB}
         turned_bank = (0, 1, 0, 1)
         acc_bank = {0: 2, 2: 0, 3: 1}
         ut_bank = (4, 5, 6, 7)
@@ -122,12 +122,10 @@ def tile_attend_spatialgate_pl_kernel(tc, first, second, ws, bias, offs, offs2, 
             nc.vector.quantize_mx(out=codes[:].bitcast(FP8X4), scales=scales[:], in_=vt_bf)
             return codes, scales
 
-        def mix(b, codes, scales, n):
+        def mix(b, codes, scales, n, k=0):
             per_bank = BANK // (4 * n)
-            banks = []
-            for k in range(PACK // per_bank):
-                acc = psum.tile([P, per_bank, n], F32, name="acc%d_%d" % (b, k), offset=(acc_bank[b] + k) * BANK)
-                banks.append(acc)
+            acc = psum.tile([P, per_bank, n], F32, name="acc%d_%d" % (b, k), offset=(acc_bank[b] + k) * BANK)
+            for once in range(1):
                 for s in range(per_bank):
                     t = k * per_bank + s
                     cols = slice(t * P, (t + 1) * P)
@@ -140,7 +138,7 @@ def tile_attend_spatialgate_pl_kernel(tc, first, second, ws, bias, offs, offs2, 
                         start=True,
                         stop=True,
                     )
-            return banks
+            return acc
 
         def add_bias(vb, acc, t_from, on_vector):
             count, n = acc.shape[1], acc.shape[2]
@@ -158,12 +156,18 @@ def tile_attend_spatialgate_pl_kernel(tc, first, second, ws, bias, offs, offs2, 
         def gather_first(b):
             u_cols = rows.tile([P, J], F32, name="u_cols%d" % b, offset=u_at[b], align_bytes=64)
             cut = F_SCALAR[b]
-            nc.scalar.activation(u_cols[:, : cut * 16], f_rows[b][:].indirect(places[:, :cut]), ACT.Copy)
-            if cut < J // 16:
-                nc.vector.tensor_copy(u_cols[:, cut * 16 :], f_rows[b][:].indirect(places[:, cut:]))
+            if cut == 0:
+                dealt = u_cols[:].bitcast(U32).rearrange("p (t m) -> p m t", t=PACK)
+                nc.vector.tensor_copy(dealt, f_rows[b][:].bitcast(U32).indirect(places[:]))
+                columns = [u_cols[:, t * P : (t + 1) * P] for t in range(PACK)]
+            else:
+                nc.scalar.activation(u_cols[:, : cut * 16], f_rows[b][:].indirect(places[:, :cut]), ACT.Copy)
+                if cut < J // 16:
+                    nc.vector.tensor_copy(u_cols[:, cut * 16 :], f_rows[b][:].indirect(places[:, cut:]))
+                columns = [u_cols[:, t:J:PACK] for t in range(PACK)]
             ut = psum.tile([P, PACK, P], F32, name="ut%d" % b, offset=ut_bank[b] * BANK)
             for t in range(PACK):
-                nc.tensor.transpose(ut[:, t, :], u_cols[:, t:J:PACK], ident[:])
+                nc.tensor.transpose(ut[:, t, :], columns[t], ident[:])
             return ut
 
         ys = [keep.tile([P, PACK, P], F32, name="y%d" % b) for b in range(BLOCKS)]
@@ -208,8 +212,9 @@ def tile_attend_spatialgate_pl_kernel(tc, first, second, ws, bias, offs, offs2, 
         nc.vector.quantize_mx(
             out=w_codes[:].bitcast(FP8X4), scales=w_scales[:], in_=w_bf[:].rearrange("p t m r -> p (t m r)")
         )
-        a01 = mix(0, *q01, 2 * P)
+        a01 = [mix(0, *q01, 2 * P, 0)]
         t2 = gather_second(2)
+        a01.append(mix(0, *q01, 2 * P, 1))
         t3 = gather_second(3)
         vt2 = copy_turned(2, t2)
         vb01 = vb_tile(0, 2 * P)
@@ -221,7 +226,7 @@ def tile_attend_spatialgate_pl_kernel(tc, first, second, ws, bias, offs, offs2, 
         a3 = mix(3, *quantize_vt(3, vt3, P), P)
         u1 = gather_first(1)
         vb2 = vb_tile(2, P)
-        add_bias(vb2, a2[0], 0, True)
+        add_bias(vb2, a2, 0, False)
         u2 = gather_first(2)
         whole = slice(0, P)
         halves = (slice(0, P // 2), slice(P // 2, P))
@@ -230,7 +235,7 @@ def tile_attend_spatialgate_pl_kernel(tc, first, second, ws, bias, offs, offs2, 
         round_y(0, whole, "gpsimd")
         u3 = gather_first(3)
         vb3 = vb_tile(3, P)
-        add_bias(vb3, a3[0], 0, False)
+        add_bias(vb3, a3, 0, False)
         gate(1, u1, vb01[:, :, P:], whole)
         store_y(1)
         gate(2, u2, vb2, whole)

@@ -24,7 +24,9 @@ ROW = T * 4
 BANK = 2048
 W_SCALAR = (32, 12)
 S_SCALAR = (0, 0, 26, 16)
-F_SCALAR = (0, 32, 0, 24)
+F_SCALAR = (22, 14, 32, 24)
+DEALT = 2
+F_ORDER = (0, 2, 1, 3)
 KB = 1024
 
 
@@ -53,14 +55,16 @@ def tile_attend_spatialgate_pl_kernel(tc, first, second, ws, bias, offs, offs2, 
         s_rows = [keep.tile([P, T], F32, name="s_rows%d" % b) for b in range(BLOCKS)]
         f_rows = [rows.tile([P, T], F32, name="f_rows%d" % b, offset=b * ROW, align_bytes=64) for b in range(BLOCKS)]
         picked_at = (32 * KB, 36 * KB, 24 * KB, 35 * KB)
-        vt_at = (40 * KB, 41 * KB, 42 * KB, 45 * KB)
-        codes_at = {0: 47 * KB, 2: 48 * KB, 3: 51 * KB}
-        u_at = (vt_at[2], picked_at[3], vt_at[3], vt_at[2])
-        vb_at = {0: 16 * KB, 2: 52 * KB, 3: 3 * ROW + 2 * KB}
+        vt_at = (40 * KB, 44 * KB)
+        codes_at = {0: 47 * KB, 2: 37 * KB}
+        u_at = (picked_at[2], vt_at[1], picked_at[3], 36 * KB)
+        vb_at = {0: 16 * KB, 2: 52 * KB}
         turned_bank = (0, 1, 0, 1)
-        acc_bank = {0: 2, 2: 0, 3: 1}
-        ut_bank = (4, 5, 6, 7)
-        vt_pair = rows.tile([P, 2 * P * PACK], BF16, name="vt_pair", offset=vt_at[0], align_bytes=64)
+        acc_bank = {0: 2, 2: 0}
+        ut_bank = (((4, range(4)),), ((5, range(4)),), ((6, range(4)),), ((7, range(3)), (4, range(3, 4))))
+        vt_pairs = [
+            rows.tile([P, 2 * P * PACK], BF16, name="vt_pair%d" % h, offset=vt_at[h], align_bytes=64) for h in range(2)
+        ]
 
         make_identity(nc, ident[:])
 
@@ -84,7 +88,7 @@ def tile_attend_spatialgate_pl_kernel(tc, first, second, ws, bias, offs, offs2, 
         load_s(3)
         nc.sync.dma_start(bias_cols[:], bias.rearrange("(p t) one -> p (t one)", t=PACK))
         nc.sync.dma_start(places[:], offs2)
-        for b in range(BLOCKS):
+        for b in F_ORDER:
             load_f(b)
 
         def round_ws(h):
@@ -107,14 +111,9 @@ def tile_attend_spatialgate_pl_kernel(tc, first, second, ws, bias, offs, offs2, 
                 nc.tensor.transpose(turned[:, u, :], words[:, u : I // 2 : 2], ident[:])
             return turned
 
-        def copy_turned(b, turned):
-            if b < 2:
-                vt_bf = vt_pair[:, b * P * PACK : (b + 1) * P * PACK]
-            else:
-                vt_tile = rows.tile([P, P * PACK], BF16, name="vt_bf%d" % b, offset=vt_at[b], align_bytes=64)
-                vt_bf = vt_tile[:]
-            nc.scalar.copy(vt_bf.bitcast(F32).rearrange("p (e u) -> p e u", u=2), turned[:].rearrange("p u e -> p e u"))
-            return vt_bf
+        def copy_turned(b, turned, copy):
+            vt_bf = vt_pairs[b // 2][:, (b % 2) * P * PACK : (b % 2 + 1) * P * PACK]
+            copy(vt_bf.bitcast(F32).rearrange("p (e u) -> p e u", u=2), turned[:].rearrange("p u e -> p e u"))
 
         def quantize_vt(b, vt_bf, n):
             codes = rows.tile([P, n], U32, name="vt_codes%d" % b, offset=codes_at[b], align_bytes=64)
@@ -156,26 +155,43 @@ def tile_attend_spatialgate_pl_kernel(tc, first, second, ws, bias, offs, offs2, 
         def gather_first(b):
             u_cols = rows.tile([P, J], F32, name="u_cols%d" % b, offset=u_at[b], align_bytes=64)
             cut = F_SCALAR[b]
-            if cut == 0:
-                dealt = u_cols[:].bitcast(U32).rearrange("p (t m) -> p m t", t=PACK)
-                nc.vector.tensor_copy(dealt, f_rows[b][:].bitcast(U32).indirect(places[:]))
-                columns = [u_cols[:, t * P : (t + 1) * P] for t in range(PACK)]
-            else:
+            if cut > 0:
                 nc.scalar.activation(u_cols[:, : cut * 16], f_rows[b][:].indirect(places[:, :cut]), ACT.Copy)
-                if cut < J // 16:
-                    nc.vector.tensor_copy(u_cols[:, cut * 16 :], f_rows[b][:].indirect(places[:, cut:]))
+            if cut < J // 16:
+                nc.vector.tensor_copy(u_cols[:, cut * 16 :], f_rows[b][:].indirect(places[:, cut:]))
+            if b == DEALT:
+                dealt = keep.tile([P, PACK, P], F32, name="u_dealt%d" % b)
+                nc.gpsimd.tensor_scalar(
+                    dealt[:].rearrange("p t (c i) -> p c t i", i=4),
+                    u_cols[:].rearrange("p (c i t) -> p c t i", i=4, t=PACK),
+                    1.0,
+                    -0.0,
+                    ALU.mult,
+                    ALU.add,
+                )
+                columns = [dealt[:, t, :] for t in range(PACK)]
+            else:
                 columns = [u_cols[:, t:J:PACK] for t in range(PACK)]
-            ut = psum.tile([P, PACK, P], F32, name="ut%d" % b, offset=ut_bank[b] * BANK)
-            for t in range(PACK):
-                nc.tensor.transpose(ut[:, t, :], columns[t], ident[:])
-            return ut
+            return columns
+
+        def turn_first(b, columns):
+            uts = []
+            for bank, ts in ut_bank[b]:
+                ut = psum.tile([P, len(ts), P], F32, name="ut%d_%d" % (b, bank), offset=bank * BANK)
+                uts.append((ut, slice(ts.start, ts.stop)))
+                for t in ts:
+                    nc.tensor.transpose(ut[:, t - ts.start, :], columns[t], ident[:])
+            return uts
 
         ys = [keep.tile([P, PACK, P], F32, name="y%d" % b) for b in range(BLOCKS)]
         out_rows = out_0.rearrange("(p t) e -> p t e", t=PACK)
         word_rows = out_1.rearrange("z p c r -> p (z c r)").bitcast(I32)
 
-        def gate(b, ut, vb, cols):
-            nc.vector.tensor_tensor(ys[b][:, :, cols], ut[:, :, cols], vb[:, :, cols], ALU.mult)
+        def gate(b, uts, vb):
+            for ut, ts in uts:
+                e0 = (b % 2) * P
+                nc.vector.tensor_tensor(ys[b][:, ts, :], ut[:], vb[:, ts, e0 : e0 + P], ALU.mult)
+            nc.sync.dma_start(out_rows[:, :, b * P : (b + 1) * P], ys[b][:])
 
         def round_y(b, cols, engine):
             c0 = (b * P + cols.start) * PACK
@@ -187,9 +203,6 @@ def tile_attend_spatialgate_pl_kernel(tc, first, second, ws, bias, offs, offs2, 
                 nc.vector.tensor_copy(dst, src)
             else:
                 nc.scalar.copy(dst, src)
-
-        def store_y(b):
-            nc.sync.dma_start(out_rows[:, :, b * P : (b + 1) * P], ys[b][:])
 
         def planes(b_from, b_to):
             cols = slice(b_from * P, b_to * P)
@@ -204,52 +217,51 @@ def tile_attend_spatialgate_pl_kernel(tc, first, second, ws, bias, offs, offs2, 
 
         t0 = gather_second(0)
         t1 = gather_second(1)
-        copy_turned(0, t0)
+        copy_turned(0, t0, nc.scalar.copy)
         round_ws(0)
-        copy_turned(1, t1)
+        copy_turned(1, t1, nc.scalar.copy)
         round_ws(1)
-        q01 = quantize_vt(0, vt_pair[:], 2 * P)
+        q01 = quantize_vt(0, vt_pairs[0][:], 2 * P)
         nc.vector.quantize_mx(
             out=w_codes[:].bitcast(FP8X4), scales=w_scales[:], in_=w_bf[:].rearrange("p t m r -> p (t m r)")
         )
         a01 = [mix(0, *q01, 2 * P, 0)]
         t2 = gather_second(2)
-        a01.append(mix(0, *q01, 2 * P, 1))
         t3 = gather_second(3)
-        vt2 = copy_turned(2, t2)
+        a01.append(mix(0, *q01, 2 * P, 1))
         vb01 = vb_tile(0, 2 * P)
         add_bias(vb01, a01[0], 0, True)
-        add_bias(vb01, a01[1], 2, False)
-        a2 = mix(2, *quantize_vt(2, vt2, P), P)
-        vt3 = copy_turned(3, t3)
-        u0 = gather_first(0)
-        a3 = mix(3, *quantize_vt(3, vt3, P), P)
-        u1 = gather_first(1)
-        vb2 = vb_tile(2, P)
-        add_bias(vb2, a2, 0, False)
-        u2 = gather_first(2)
+        copy_turned(2, t2, nc.vector.tensor_copy)
+        c0 = gather_first(0)
+        copy_turned(3, t3, nc.scalar.copy)
+        u0 = turn_first(0, c0)
+        q23 = quantize_vt(2, vt_pairs[1][:], 2 * P)
+        a23 = [mix(2, *q23, 2 * P, k) for k in range(2)]
+        c2 = gather_first(2)
+        add_bias(vb01, a01[1], 2, True)
+        c1 = gather_first(1)
+        u2 = turn_first(2, c2)
+        u1 = turn_first(1, c1)
         whole = slice(0, P)
         halves = (slice(0, P // 2), slice(P // 2, P))
-        gate(0, u0, vb01[:, :, :P], whole)
-        store_y(0)
+        gate(0, u0, vb01)
         round_y(0, whole, "gpsimd")
-        u3 = gather_first(3)
-        vb3 = vb_tile(3, P)
-        add_bias(vb3, a3, 0, False)
-        gate(1, u1, vb01[:, :, P:], whole)
-        store_y(1)
-        gate(2, u2, vb2, whole)
-        store_y(2)
-        round_y(1, whole, "vector")
+        vb23 = vb_tile(2, 2 * P)
+        add_bias(vb23, a23[0], 0, False)
+        u3 = turn_first(3, gather_first(3))
+        add_bias(vb23, a23[1], 2, True)
+        gate(1, u1, vb01)
+        round_y(1, whole, "scalar")
+        gate(2, u2, vb23)
         round_y(2, whole, "scalar")
-        for cols in halves:
-            gate(3, u3, vb3, cols)
-            round_y(3, cols, "scalar")
-        store_y(3)
-        planes(0, 3)
-        store_words(0, 3 * P)
+        gate(3, u3, vb23)
+        round_y(3, halves[0], "scalar")
+        planes(0, 2)
+        store_words(0, 2 * P)
+        round_y(3, halves[1], "vector")
+        planes(2, 3)
         planes(3, 4)
-        store_words(3 * P, 4 * P)
+        store_words(2 * P, 4 * P)
 
         scale_rows = out_2.rearrange("z q c -> (z q) c").bitcast(I32)
         for quad in range(4):

@@ -22,11 +22,9 @@ BLOCKS = E // P
 W_PIECES = 2
 ROW = T * 4
 BANK = 2048
-W_SCALAR = (32, 12)
+W_SCALAR = (32, 48)
 S_SCALAR = (0, 0, 26, 16)
-F_SCALAR = (22, 14, 32, 24)
-DEALT = 2
-F_ORDER = (0, 2, 1, 3)
+F_SCALAR = (0, 32, 0, 24)
 KB = 1024
 
 
@@ -56,12 +54,12 @@ def tile_attend_spatialgate_pl_kernel(tc, first, second, ws, bias, offs, offs2, 
         f_rows = [rows.tile([P, T], F32, name="f_rows%d" % b, offset=b * ROW, align_bytes=64) for b in range(BLOCKS)]
         picked_at = (32 * KB, 36 * KB, 24 * KB, 35 * KB)
         vt_at = (40 * KB, 44 * KB)
-        codes_at = {0: 47 * KB, 2: 37 * KB}
-        u_at = (picked_at[2], vt_at[1], picked_at[3], 36 * KB)
-        vb_at = {0: 16 * KB, 2: 52 * KB}
+        codes_at = {0: 47 * KB, 2: 38 * KB}
+        u_at = (picked_at[2], picked_at[3], picked_at[2], 37 * KB)
+        vb_at = {0: 16 * KB, 2: 52 * KB, 3: 54 * KB}
         turned_bank = (0, 1, 0, 1)
-        acc_bank = {0: 2, 2: 0}
-        ut_bank = (((4, range(4)),), ((5, range(4)),), ((6, range(4)),), ((7, range(3)), (4, range(3, 4))))
+        acc_bank = {0: 2, 2: 0, 3: 1}
+        ut_bank = (((4, range(4)),), ((5, range(4)),), ((6, range(4)),), ((7, range(3)), (2, range(3, 4))))
         vt_pairs = [
             rows.tile([P, 2 * P * PACK], BF16, name="vt_pair%d" % h, offset=vt_at[h], align_bytes=64) for h in range(2)
         ]
@@ -88,15 +86,24 @@ def tile_attend_spatialgate_pl_kernel(tc, first, second, ws, bias, offs, offs2, 
         load_s(3)
         nc.sync.dma_start(bias_cols[:], bias.rearrange("(p t) one -> p (t one)", t=PACK))
         nc.sync.dma_start(places[:], offs2)
-        for b in F_ORDER:
+        for b in range(BLOCKS):
             load_f(b)
 
-        def round_ws(h):
-            mw = wj // PACK
-            for copy, m_from, m_to in ((nc.scalar.copy, 0, W_SCALAR[h]), (nc.vector.tensor_copy, W_SCALAR[h], mw)):
-                dst = w_bf[:, :, h * mw + m_from : h * mw + m_to, :].rearrange("p t m r -> p m r t")
-                src = w_raw[h][:, :, m_from * PACK : m_to * PACK].rearrange("p r (m t) -> p m r t", t=PACK)
-                copy(dst, src)
+        mw = wj // PACK
+
+        def round_ws(copy, h, ms, ts):
+            copy(
+                w_bf[:, ts, h * mw + ms.start : h * mw + ms.stop, :].rearrange("p t m r -> p m r t"),
+                w_raw[h][:].rearrange("p r (m t) -> p m r t", t=PACK)[:, ms, :, ts],
+            )
+
+        def quantize_ws(ts):
+            cols = slice(ts.start * P, ts.stop * P)
+            nc.vector.quantize_mx(
+                out=w_codes[:, cols].bitcast(FP8X4),
+                scales=w_scales[:, cols],
+                in_=w_bf[:, ts, :, :].rearrange("p t m r -> p (t m r)"),
+            )
 
         def gather_second(b):
             picked = rows.tile([P, I], BF16, name="picked%d" % b, offset=picked_at[b], align_bytes=64)
@@ -121,7 +128,7 @@ def tile_attend_spatialgate_pl_kernel(tc, first, second, ws, bias, offs, offs2, 
             nc.vector.quantize_mx(out=codes[:].bitcast(FP8X4), scales=scales[:], in_=vt_bf)
             return codes, scales
 
-        def mix(b, codes, scales, n, k=0):
+        def mix(b, codes, scales, n, k=0, e0=0):
             per_bank = BANK // (4 * n)
             acc = psum.tile([P, per_bank, n], F32, name="acc%d_%d" % (b, k), offset=(acc_bank[b] + k) * BANK)
             for once in range(1):
@@ -132,8 +139,8 @@ def tile_attend_spatialgate_pl_kernel(tc, first, second, ws, bias, offs, offs2, 
                         out=acc[:, s, :],
                         lhsT=w_codes[:, cols].bitcast(FP8X4),
                         lhsT_scale=w_scales[:, cols],
-                        rhs=codes[:].bitcast(FP8X4),
-                        rhs_scale=scales[:],
+                        rhs=codes[:, e0 : e0 + n].bitcast(FP8X4),
+                        rhs_scale=scales[:, e0 : e0 + n],
                         start=True,
                         stop=True,
                     )
@@ -155,24 +162,14 @@ def tile_attend_spatialgate_pl_kernel(tc, first, second, ws, bias, offs, offs2, 
         def gather_first(b):
             u_cols = rows.tile([P, J], F32, name="u_cols%d" % b, offset=u_at[b], align_bytes=64)
             cut = F_SCALAR[b]
-            if cut > 0:
-                nc.scalar.activation(u_cols[:, : cut * 16], f_rows[b][:].indirect(places[:, :cut]), ACT.Copy)
+            if cut == 0:
+                dealt = u_cols[:].bitcast(U32).rearrange("p (t m) -> p m t", t=PACK)
+                nc.vector.tensor_copy(dealt, f_rows[b][:].bitcast(U32).indirect(places[:]))
+                return [u_cols[:, t * P : (t + 1) * P] for t in range(PACK)]
+            nc.scalar.activation(u_cols[:, : cut * 16], f_rows[b][:].indirect(places[:, :cut]), ACT.Copy)
             if cut < J // 16:
                 nc.vector.tensor_copy(u_cols[:, cut * 16 :], f_rows[b][:].indirect(places[:, cut:]))
-            if b == DEALT:
-                dealt = keep.tile([P, PACK, P], F32, name="u_dealt%d" % b)
-                nc.gpsimd.tensor_scalar(
-                    dealt[:].rearrange("p t (c i) -> p c t i", i=4),
-                    u_cols[:].rearrange("p (c i t) -> p c t i", i=4, t=PACK),
-                    1.0,
-                    -0.0,
-                    ALU.mult,
-                    ALU.add,
-                )
-                columns = [dealt[:, t, :] for t in range(PACK)]
-            else:
-                columns = [u_cols[:, t:J:PACK] for t in range(PACK)]
-            return columns
+            return [u_cols[:, t:J:PACK] for t in range(PACK)]
 
         def turn_first(b, columns):
             uts = []
@@ -189,7 +186,7 @@ def tile_attend_spatialgate_pl_kernel(tc, first, second, ws, bias, offs, offs2, 
 
         def gate(b, uts, vb):
             for ut, ts in uts:
-                e0 = (b % 2) * P
+                e0 = P if b == 1 else 0
                 nc.vector.tensor_tensor(ys[b][:, ts, :], ut[:], vb[:, ts, e0 : e0 + P], ALU.mult)
             nc.sync.dma_start(out_rows[:, :, b * P : (b + 1) * P], ys[b][:])
 
@@ -198,7 +195,8 @@ def tile_attend_spatialgate_pl_kernel(tc, first, second, ws, bias, offs, offs2, 
             dst = y_bf[:, c0 : c0 + (cols.stop - cols.start) * PACK].rearrange("p (c i t) -> p c t i", i=4, t=PACK)
             src = ys[b][:, :, cols].rearrange("p t (c i) -> p c t i", i=4)
             if engine == "gpsimd":
-                nc.gpsimd.tensor_scalar(dst, src, 1.0, -0.0, ALU.mult, ALU.add)
+                words = y_bf[:, c0 : c0 + P * PACK].rearrange("p (c t) -> p c t", t=PACK)
+                nc.gpsimd.tensor_scalar(words, ys[b][:].rearrange("p t c -> p c t"), 1.0, -0.0, ALU.mult, ALU.add)
             elif engine == "vector":
                 nc.vector.tensor_copy(dst, src)
             else:
@@ -217,51 +215,50 @@ def tile_attend_spatialgate_pl_kernel(tc, first, second, ws, bias, offs, offs2, 
 
         t0 = gather_second(0)
         t1 = gather_second(1)
+        low, high, every = slice(0, 2), slice(2, PACK), slice(0, PACK)
         copy_turned(0, t0, nc.scalar.copy)
-        round_ws(0)
+        round_ws(nc.scalar.copy, 0, slice(0, W_SCALAR[0]), every)
+        round_ws(nc.vector.tensor_copy, 0, slice(W_SCALAR[0], mw), every)
         copy_turned(1, t1, nc.scalar.copy)
-        round_ws(1)
+        round_ws(nc.vector.tensor_copy, 1, slice(0, mw), low)
+        round_ws(nc.vector.tensor_copy, 1, slice(W_SCALAR[1], mw), high)
+        round_ws(nc.scalar.copy, 1, slice(0, W_SCALAR[1]), high)
         q01 = quantize_vt(0, vt_pairs[0][:], 2 * P)
-        nc.vector.quantize_mx(
-            out=w_codes[:].bitcast(FP8X4), scales=w_scales[:], in_=w_bf[:].rearrange("p t m r -> p (t m r)")
-        )
-        a01 = [mix(0, *q01, 2 * P, 0)]
+        quantize_ws(low)
+        quantize_ws(high)
+        a01 = [mix(0, *q01, 2 * P, k) for k in range(2)]
         t2 = gather_second(2)
         t3 = gather_second(3)
-        a01.append(mix(0, *q01, 2 * P, 1))
         vb01 = vb_tile(0, 2 * P)
         add_bias(vb01, a01[0], 0, True)
-        copy_turned(2, t2, nc.vector.tensor_copy)
-        c0 = gather_first(0)
+        add_bias(vb01, a01[1], 2, False)
+        copy_turned(2, t2, nc.scalar.copy)
         copy_turned(3, t3, nc.scalar.copy)
-        u0 = turn_first(0, c0)
+        u0 = turn_first(0, gather_first(0))
         q23 = quantize_vt(2, vt_pairs[1][:], 2 * P)
-        a23 = [mix(2, *q23, 2 * P, k) for k in range(2)]
-        c2 = gather_first(2)
-        add_bias(vb01, a01[1], 2, True)
-        c1 = gather_first(1)
-        u2 = turn_first(2, c2)
-        u1 = turn_first(1, c1)
+        a23 = [mix(2 + k, *q23, P, 0, k * P) for k in range(2)]
+        u1 = turn_first(1, gather_first(1))
         whole = slice(0, P)
         halves = (slice(0, P // 2), slice(P // 2, P))
         gate(0, u0, vb01)
         round_y(0, whole, "gpsimd")
-        vb23 = vb_tile(2, 2 * P)
-        add_bias(vb23, a23[0], 0, False)
+        u2 = turn_first(2, gather_first(2))
+        vb2 = vb_tile(2, P)
+        vb3 = vb_tile(3, P)
+        add_bias(vb2, a23[0], 0, False)
         u3 = turn_first(3, gather_first(3))
-        add_bias(vb23, a23[1], 2, True)
+        add_bias(vb3, a23[1], 0, False)
         gate(1, u1, vb01)
-        round_y(1, whole, "scalar")
-        gate(2, u2, vb23)
+        round_y(1, whole, "gpsimd")
+        gate(2, u2, vb2)
         round_y(2, whole, "scalar")
-        gate(3, u3, vb23)
+        gate(3, u3, vb3)
         round_y(3, halves[0], "scalar")
         planes(0, 2)
-        store_words(0, 2 * P)
         round_y(3, halves[1], "vector")
         planes(2, 3)
         planes(3, 4)
-        store_words(2 * P, 4 * P)
+        store_words(0, 4 * P)
 
         scale_rows = out_2.rearrange("z q c -> (z q) c").bitcast(I32)
         for quad in range(4):

@@ -262,7 +262,7 @@ def tile_attend_spatialgate_pl_kernel(tc, first, second, ws, bias, offs, offs2, 
 
         scale_rows = out_2.rearrange("z q c -> (z q) c").bitcast(I32)
         for quad in range(4):
-            queue = nc.sync if quad % 2 == 0 else nc.scalar
+            queue = nc.scalar
             queue.dma_start(
                 scale_rows[4 * quad : 4 * quad + 4, :], y_scales[32 * quad : 32 * quad + 4, :].bitcast(I32)
             )

@@ -22,7 +22,7 @@ BLOCKS = E // P
 W_PIECES = 2
 ROW = T * 4
 BANK = 2048
-W_SCALAR = (32, 48)
+W_SCALAR = (64, 96)
 S_SCALAR = (0, 0, 26, 16)
 F_SCALAR = (0, 32, 0, 24)
 KB = 1024
@@ -39,10 +39,9 @@ def tile_attend_spatialgate_pl_kernel(tc, first, second, ws, bias, offs, offs2, 
         places = keep.tile([P, J // 16], U16, name="places")
         bias_cols = keep.tile([P, PACK], F32, name="bias_cols")
         ident = keep.tile([P, P], F32, name="ident")
-        wj = J // W_PIECES
         w_raw = [
-            keep.tile([P, PACK, wj], F32, name="w_raw0"),
-            rows.tile([P, PACK, wj], F32, name="w_raw1", offset=24 * KB, align_bytes=64),
+            keep.tile([P, 2, J], F32, name="w_raw0"),
+            rows.tile([P, 2, J], F32, name="w_raw1", offset=24 * KB, align_bytes=64),
         ]
         w_bf = rows.tile([P, PACK, P, PACK], BF16, name="w_bf", offset=32 * KB, align_bytes=64)
         w_codes = keep.tile([P, J], U32, name="w_codes", align_bytes=64)
@@ -69,7 +68,7 @@ def tile_attend_spatialgate_pl_kernel(tc, first, second, ws, bias, offs, offs2, 
         ws_rows = ws.rearrange("(p r) j -> p r j", r=PACK)
 
         def load_w(h):
-            nc.sync.dma_start(w_raw[h][:], ws_rows[:, :, h * wj : (h + 1) * wj])
+            nc.sync.dma_start(w_raw[h][:], ws_rows[:, 2 * h : 2 * h + 2, :])
 
         def load_s(b):
             nc.sync.dma_start(s_rows[b][:], second[b * P : (b + 1) * P, :])
@@ -89,11 +88,11 @@ def tile_attend_spatialgate_pl_kernel(tc, first, second, ws, bias, offs, offs2, 
         for b in range(BLOCKS):
             load_f(b)
 
-        mw = wj // PACK
+        mw = J // PACK
 
         def round_ws(copy, h, ms, ts):
             copy(
-                w_bf[:, ts, h * mw + ms.start : h * mw + ms.stop, :].rearrange("p t m r -> p m r t"),
+                w_bf[:, ts, ms, 2 * h : 2 * h + 2].rearrange("p t m r -> p m r t"),
                 w_raw[h][:].rearrange("p r (m t) -> p m r t", t=PACK)[:, ms, :, ts],
             )
 

@@ -24,7 +24,7 @@ ROW = T * 4
 BANK = 2048
 W_SCALAR = (64, 96)
 S_SCALAR = (0, 0, 26, 16)
-F_SCALAR = (0, 32, 0, 24)
+F_SCALAR = (32, 0, 0, 24)
 KB = 1024
 
 
@@ -53,14 +53,16 @@ def tile_attend_spatialgate_pl_kernel(tc, first, second, ws, bias, offs, offs2, 
         f_rows = [rows.tile([P, T], F32, name="f_rows%d" % b, offset=b * ROW, align_bytes=64) for b in range(BLOCKS)]
         picked_at = (32 * KB, 36 * KB, 24 * KB, 35 * KB)
         vt_at = (40 * KB, 44 * KB)
-        codes_at = {0: 47 * KB, 2: 38 * KB}
-        u_at = (picked_at[2], picked_at[3], picked_at[2], 37 * KB)
+        codes_at = {0: 47 * KB, 2: 38 * KB, 3: 58 * KB}
+        u_at = (picked_at[3], 45 * KB, codes_at[3], picked_at[3])
         vb_at = {0: 16 * KB, 2: 52 * KB, 3: 54 * KB}
         turned_bank = (0, 1, 0, 1)
         acc_bank = {0: 2, 2: 0, 3: 1}
         ut_bank = (((4, range(4)),), ((5, range(4)),), ((6, range(4)),), ((7, range(3)), (2, range(3, 4))))
-        vt_pairs = [
-            rows.tile([P, 2 * P * PACK], BF16, name="vt_pair%d" % h, offset=vt_at[h], align_bytes=64) for h in range(2)
+        vt_pair = rows.tile([P, 2 * P * PACK], BF16, name="vt_pair", offset=vt_at[0], align_bytes=64)
+        vt_bfs = [vt_pair[:, : P * PACK], vt_pair[:, P * PACK :]] + [
+            rows.tile([P, P * PACK], BF16, name="vt%d" % b, offset=vt_at[1] + (b - 2) * KB, align_bytes=64)[:]
+            for b in (2, 3)
         ]
 
         make_identity(nc, ident[:])
@@ -118,7 +120,7 @@ def tile_attend_spatialgate_pl_kernel(tc, first, second, ws, bias, offs, offs2, 
             return turned
 
         def copy_turned(b, turned, copy):
-            vt_bf = vt_pairs[b // 2][:, (b % 2) * P * PACK : (b % 2 + 1) * P * PACK]
+            vt_bf = vt_bfs[b]
             copy(vt_bf.bitcast(F32).rearrange("p (e u) -> p e u", u=2), turned[:].rearrange("p u e -> p e u"))
 
         def quantize_vt(b, vt_bf, n):
@@ -222,7 +224,7 @@ def tile_attend_spatialgate_pl_kernel(tc, first, second, ws, bias, offs, offs2, 
         round_ws(nc.vector.tensor_copy, 1, slice(0, mw), low)
         round_ws(nc.vector.tensor_copy, 1, slice(W_SCALAR[1], mw), high)
         round_ws(nc.scalar.copy, 1, slice(0, W_SCALAR[1]), high)
-        q01 = quantize_vt(0, vt_pairs[0][:], 2 * P)
+        q01 = quantize_vt(0, vt_pair[:], 2 * P)
         quantize_ws(low)
         quantize_ws(high)
         a01 = [mix(0, *q01, 2 * P, k) for k in range(2)]
@@ -230,23 +232,22 @@ def tile_attend_spatialgate_pl_kernel(tc, first, second, ws, bias, offs, offs2, 
         t3 = gather_second(3)
         vb01 = vb_tile(0, 2 * P)
         add_bias(vb01, a01[0], 0, True)
-        add_bias(vb01, a01[1], 2, False)
+        add_bias(vb01, a01[1], 2, True)
         copy_turned(2, t2, nc.scalar.copy)
         copy_turned(3, t3, nc.scalar.copy)
+        a23 = [mix(b, *quantize_vt(b, vt_bfs[b], P), P) for b in (2, 3)]
         u0 = turn_first(0, gather_first(0))
-        q23 = quantize_vt(2, vt_pairs[1][:], 2 * P)
-        a23 = [mix(2 + k, *q23, P, 0, k * P) for k in range(2)]
         u1 = turn_first(1, gather_first(1))
         whole = slice(0, P)
         halves = (slice(0, P // 2), slice(P // 2, P))
-        gate(0, u0, vb01)
-        round_y(0, whole, "gpsimd")
-        u2 = turn_first(2, gather_first(2))
         vb2 = vb_tile(2, P)
         vb3 = vb_tile(3, P)
         add_bias(vb2, a23[0], 0, False)
-        u3 = turn_first(3, gather_first(3))
         add_bias(vb3, a23[1], 0, False)
+        u2 = turn_first(2, gather_first(2))
+        u3 = turn_first(3, gather_first(3))
+        gate(0, u0, vb01)
+        round_y(0, whole, "gpsimd")
         gate(1, u1, vb01)
         round_y(1, whole, "gpsimd")
         gate(2, u2, vb2)

@@ -24,7 +24,7 @@ ROW = T * 4
 BANK = 2048
 W_SCALAR = (64, 96)
 S_SCALAR = (0, 0, 26, 16)
-F_SCALAR = (32, 0, 0, 24)
+F_SCALAR = (32, 0, 12, 22)
 KB = 1024
 
 
@@ -55,7 +55,7 @@ def tile_attend_spatialgate_pl_kernel(tc, first, second, ws, bias, offs, offs2, 
         vt_at = (40 * KB, 44 * KB)
         codes_at = {0: 47 * KB, 2: 38 * KB, 3: 58 * KB}
         u_at = (picked_at[3], 45 * KB, codes_at[3], picked_at[3])
-        vb_at = {0: 16 * KB, 2: 52 * KB, 3: 54 * KB}
+        vb_at = {0: 16 * KB, 2: 52 * KB, 3: 14 * KB}
         turned_bank = (0, 1, 0, 1)
         acc_bank = {0: 2, 2: 0, 3: 1}
         ut_bank = (((4, range(4)),), ((5, range(4)),), ((6, range(4)),), ((7, range(3)), (2, range(3, 4))))
@@ -172,6 +172,19 @@ def tile_attend_spatialgate_pl_kernel(tc, first, second, ws, bias, offs, offs2, 
                 nc.vector.tensor_copy(u_cols[:, cut * 16 :], f_rows[b][:].indirect(places[:, cut:]))
             return [u_cols[:, t:J:PACK] for t in range(PACK)]
 
+        def gather_first_dealt(b):
+            u_cols = rows.tile([P, J], F32, name="u_cols%d" % b, offset=u_at[b], align_bytes=64)
+            cut = J // 16 - F_SCALAR[b]
+            plain = rows.tile([P, F_SCALAR[b] * 16], F32, name="u_plain", offset=codes_at[2], align_bytes=64)
+            dealt = u_cols[:].bitcast(U32).rearrange("p (t m) -> p m t", t=PACK)
+            nc.scalar.activation(plain[:], f_rows[b][:].indirect(places[:, cut:]), ACT.Copy)
+            nc.vector.tensor_copy(dealt[:, : cut * 4, :], f_rows[b][:].bitcast(U32).indirect(places[:, :cut]))
+            nc.vector.tensor_copy(
+                u_cols[:].rearrange("p (t c i) -> p c t i", t=PACK, i=4)[:, cut:, :, :],
+                plain[:].rearrange("p (c i t) -> p c t i", t=PACK, i=4),
+            )
+            return [u_cols[:, t * P : (t + 1) * P] for t in range(PACK)]
+
         def turn_first(b, columns):
             uts = []
             for bank, ts in ut_bank[b]:
@@ -239,13 +252,13 @@ def tile_attend_spatialgate_pl_kernel(tc, first, second, ws, bias, offs, offs2, 
         u0 = turn_first(0, gather_first(0))
         u1 = turn_first(1, gather_first(1))
         whole = slice(0, P)
-        halves = (slice(0, P // 2), slice(P // 2, P))
+        halves = (slice(0, 64), slice(64, P))
         vb2 = vb_tile(2, P)
         vb3 = vb_tile(3, P)
         add_bias(vb2, a23[0], 0, False)
-        add_bias(vb3, a23[1], 0, False)
-        u2 = turn_first(2, gather_first(2))
+        u2 = turn_first(2, gather_first_dealt(2))
         u3 = turn_first(3, gather_first(3))
+        add_bias(vb3, a23[1], 0, False)
         gate(0, u0, vb01)
         round_y(0, whole, "gpsimd")
         gate(1, u1, vb01)

@@ -24,7 +24,7 @@ ROW = T * 4
 BANK = 2048
 W_SCALAR = (64, 96)
 S_SCALAR = (0, 0, 26, 16)
-F_SCALAR = (32, 0, 12, 22)
+F_SCALAR = (10, 12, 12, 22)
 KB = 1024
 
 
@@ -54,7 +54,8 @@ def tile_attend_spatialgate_pl_kernel(tc, first, second, ws, bias, offs, offs2, 
         picked_at = (32 * KB, 36 * KB, 24 * KB, 35 * KB)
         vt_at = (40 * KB, 44 * KB)
         codes_at = {0: 47 * KB, 2: 38 * KB, 3: 58 * KB}
-        u_at = (picked_at[3], 45 * KB, codes_at[3], picked_at[3])
+        u_at = (32 * KB, 45 * KB, codes_at[3], 32 * KB)
+        plain_at = (picked_at[3], vt_at[1], codes_at[2])
         vb_at = {0: 16 * KB, 2: 52 * KB, 3: 14 * KB}
         turned_bank = (0, 1, 0, 1)
         acc_bank = {0: 2, 2: 0, 3: 1}
@@ -175,10 +176,13 @@ def tile_attend_spatialgate_pl_kernel(tc, first, second, ws, bias, offs, offs2, 
         def gather_first_dealt(b):
             u_cols = rows.tile([P, J], F32, name="u_cols%d" % b, offset=u_at[b], align_bytes=64)
             cut = J // 16 - F_SCALAR[b]
-            plain = rows.tile([P, F_SCALAR[b] * 16], F32, name="u_plain", offset=codes_at[2], align_bytes=64)
+            plain = rows.tile([P, F_SCALAR[b] * 16], F32, name="u_plain%d" % b, offset=plain_at[b], align_bytes=64)
             dealt = u_cols[:].bitcast(U32).rearrange("p (t m) -> p m t", t=PACK)
             nc.scalar.activation(plain[:], f_rows[b][:].indirect(places[:, cut:]), ACT.Copy)
             nc.vector.tensor_copy(dealt[:, : cut * 4, :], f_rows[b][:].bitcast(U32).indirect(places[:, :cut]))
+            return u_cols, plain, cut
+
+        def deal_rest(u_cols, plain, cut):
             nc.vector.tensor_copy(
                 u_cols[:].rearrange("p (t c i) -> p c t i", t=PACK, i=4)[:, cut:, :, :],
                 plain[:].rearrange("p (c i t) -> p c t i", t=PACK, i=4),
@@ -245,18 +249,19 @@ def tile_attend_spatialgate_pl_kernel(tc, first, second, ws, bias, offs, offs2, 
         t3 = gather_second(3)
         vb01 = vb_tile(0, 2 * P)
         add_bias(vb01, a01[0], 0, True)
-        add_bias(vb01, a01[1], 2, True)
+        add_bias(vb01, a01[1], 2, False)
         copy_turned(2, t2, nc.scalar.copy)
         copy_turned(3, t3, nc.scalar.copy)
+        g0 = gather_first_dealt(0)
         a23 = [mix(b, *quantize_vt(b, vt_bfs[b], P), P) for b in (2, 3)]
-        u0 = turn_first(0, gather_first(0))
-        u1 = turn_first(1, gather_first(1))
+        u0 = turn_first(0, deal_rest(*g0))
+        u1 = turn_first(1, deal_rest(*gather_first_dealt(1)))
         whole = slice(0, P)
         halves = (slice(0, 64), slice(64, P))
         vb2 = vb_tile(2, P)
         vb3 = vb_tile(3, P)
         add_bias(vb2, a23[0], 0, False)
-        u2 = turn_first(2, gather_first_dealt(2))
+        u2 = turn_first(2, deal_rest(*gather_first_dealt(2)))
         u3 = turn_first(3, gather_first(3))
         add_bias(vb3, a23[1], 0, False)
         gate(0, u0, vb01)

@@ -24,7 +24,8 @@ ROW = T * 4
 BANK = 2048
 W_SCALAR = (64, 96)
 S_SCALAR = (0, 0, 26, 16)
-F_SCALAR = (10, 12, 12, 22)
+F_SCALAR = (0, 32, 8, 22)
+F_EARLY = 24
 KB = 1024
 
 
@@ -54,17 +55,17 @@ def tile_attend_spatialgate_pl_kernel(tc, first, second, ws, bias, offs, offs2, 
         picked_at = (32 * KB, 36 * KB, 24 * KB, 35 * KB)
         vt_at = (40 * KB, 44 * KB)
         codes_at = {0: 47 * KB, 2: 38 * KB, 3: 58 * KB}
-        u_at = (32 * KB, 45 * KB, codes_at[3], 32 * KB)
+        u_at = (32 * KB, picked_at[3], 45 * KB, 32 * KB)
         plain_at = (picked_at[3], vt_at[1], codes_at[2])
         vb_at = {0: 16 * KB, 2: 52 * KB, 3: 14 * KB}
         turned_bank = (0, 1, 0, 1)
         acc_bank = {0: 2, 2: 0, 3: 1}
         ut_bank = (((4, range(4)),), ((5, range(4)),), ((6, range(4)),), ((7, range(3)), (2, range(3, 4))))
         vt_pair = rows.tile([P, 2 * P * PACK], BF16, name="vt_pair", offset=vt_at[0], align_bytes=64)
-        vt_bfs = [vt_pair[:, : P * PACK], vt_pair[:, P * PACK :]] + [
-            rows.tile([P, P * PACK], BF16, name="vt%d" % b, offset=vt_at[1] + (b - 2) * KB, align_bytes=64)[:]
-            for b in (2, 3)
-        ]
+        vt2_at = 3 * P + F_EARLY * 4
+        u_first = rows.tile([P, vt2_at + 2 * P], F32, name="u_first", offset=u_at[0], align_bytes=64)
+        vt3 = rows.tile([P, P * PACK], BF16, name="vt3", offset=45 * KB, align_bytes=64)
+        vt_bfs = [vt_pair[:, : P * PACK], vt_pair[:, P * PACK :], u_first[:, vt2_at:].bitcast(BF16), vt3[:]]
 
         make_identity(nc, ident[:])
 
@@ -173,6 +174,11 @@ def tile_attend_spatialgate_pl_kernel(tc, first, second, ws, bias, offs, offs2, 
                 nc.vector.tensor_copy(u_cols[:, cut * 16 :], f_rows[b][:].indirect(places[:, cut:]))
             return [u_cols[:, t:J:PACK] for t in range(PACK)]
 
+        def gather_part(c_from, c_to):
+            dealt = u_first[:, :J].bitcast(U32).rearrange("p (t m) -> p m t", t=PACK)
+            window = f_rows[0][:].bitcast(U32).indirect(places[:, c_from:c_to])
+            nc.vector.tensor_copy(dealt[:, c_from * 4 : c_to * 4, :], window)
+
         def gather_first_dealt(b):
             u_cols = rows.tile([P, J], F32, name="u_cols%d" % b, offset=u_at[b], align_bytes=64)
             cut = J // 16 - F_SCALAR[b]
@@ -252,10 +258,12 @@ def tile_attend_spatialgate_pl_kernel(tc, first, second, ws, bias, offs, offs2, 
         add_bias(vb01, a01[1], 2, False)
         copy_turned(2, t2, nc.scalar.copy)
         copy_turned(3, t3, nc.scalar.copy)
-        g0 = gather_first_dealt(0)
-        a23 = [mix(b, *quantize_vt(b, vt_bfs[b], P), P) for b in (2, 3)]
-        u0 = turn_first(0, deal_rest(*g0))
-        u1 = turn_first(1, deal_rest(*gather_first_dealt(1)))
+        gather_part(0, F_EARLY)
+        a23 = [mix(2, *quantize_vt(2, vt_bfs[2], P), P)]
+        gather_part(F_EARLY, J // 16)
+        a23.append(mix(3, *quantize_vt(3, vt_bfs[3], P), P))
+        u0 = turn_first(0, [u_first[:, t * P : (t + 1) * P] for t in range(PACK)])
+        u1 = turn_first(1, gather_first(1))
         whole = slice(0, P)
         halves = (slice(0, 64), slice(64, P))
         vb2 = vb_tile(2, P)

from contextlib import ExitStack

import concourse.mybir as mybir
from concourse.masks import make_identity

E, T, I, J = 512, 1024, 512, 512
FLOPS = 2 * I * J * E

F32 = mybir.dt.float32
BF16 = mybir.dt.bfloat16
I32 = mybir.dt.int32
U32 = mybir.dt.uint32
U16 = mybir.dt.uint16
U8 = mybir.dt.uint8
FP8X4 = mybir.dt.float8_e4m3fn_x4
ACT = mybir.ActivationFunctionType
ALU = mybir.AluOpType

P = 128
PACK = 4
BLOCKS = E // P
W_PIECES = 2
ROW = T * 4
BANK = 2048
W_SCALAR = (64, 96)
S_SCALAR = (0, 0, 26, 16)
F_SCALAR = (0, 32, 8, 22)
F_EARLY = 24
KB = 1024


def tile_attend_spatialgate_pl_kernel(tc, first, second, ws, bias, offs, offs2, out_0, out_1, out_2):
    nc = tc.nc
    with ExitStack() as ctx:
        keep = ctx.enter_context(tc.tile_pool(name="keep", bufs=1))
        rows = ctx.enter_context(tc.tile_pool(name="rows", bufs=1))
        psum = ctx.enter_context(tc.psum_pool(name="psum", bufs=1))

        slots = keep.tile([P, I // 16], U16, name="slots")
        places = keep.tile([P, J // 16], U16, name="places")
        bias_cols = keep.tile([P, PACK], F32, name="bias_cols")
        ident = keep.tile([P, P], F32, name="ident")
        w_raw = [
            keep.tile([P, 2, J], F32, name="w_raw0"),
            rows.tile([P, 2, J], F32, name="w_raw1", offset=24 * KB, align_bytes=64),
        ]
        w_bf = rows.tile([P, PACK, P, PACK], BF16, name="w_bf", offset=32 * KB, align_bytes=64)
        w_codes = keep.tile([P, J], U32, name="w_codes", align_bytes=64)
        w_scales = keep.tile([P, J], U8, name="w_scales", align_bytes=64)
        y_bf = keep.tile([P, E * PACK], BF16, name="y_bf", align_bytes=64)
        y_codes = rows.tile([P, E], U32, name="y_codes", offset=3 * ROW, align_bytes=64)
        y_scales = keep.tile([P, E], U8, name="y_scales", align_bytes=64)
        s_rows = [keep.tile([P, T], F32, name="s_rows%d" % b) for b in range(BLOCKS)]
        f_rows = [rows.tile([P, T], F32, name="f_rows%d" % b, offset=b * ROW, align_bytes=64) for b in range(BLOCKS)]
        picked_at = (32 * KB, 36 * KB, 24 * KB, 35 * KB)
        vt_at = (40 * KB, 44 * KB)
        codes_at = {0: 47 * KB, 2: 38 * KB, 3: 58 * KB}
        u_at = (32 * KB, picked_at[3], 45 * KB, 32 * KB)
        plain_at = (picked_at[3], vt_at[1], codes_at[2])
        vb_at = {0: 16 * KB, 2: 52 * KB, 3: 14 * KB}
        turned_bank = (0, 1, 0, 1)
        acc_bank = {0: 2, 2: 0, 3: 1}
        ut_bank = (((4, range(4)),), ((5, range(4)),), ((6, range(4)),), ((7, range(3)), (2, range(3, 4))))
        vt_pair = rows.tile([P, 2 * P * PACK], BF16, name="vt_pair", offset=vt_at[0], align_bytes=64)
        vt2_at = 3 * P + F_EARLY * 4
        u_first = rows.tile([P, vt2_at + 2 * P], F32, name="u_first", offset=u_at[0], align_bytes=64)
        vt3 = rows.tile([P, P * PACK], BF16, name="vt3", offset=45 * KB, align_bytes=64)
        vt_bfs = [vt_pair[:, : P * PACK], vt_pair[:, P * PACK :], u_first[:, vt2_at:].bitcast(BF16), vt3[:]]

        make_identity(nc, ident[:])

        ws_rows = ws.rearrange("(p r) j -> p r j", r=PACK)

        def load_w(h):
            nc.sync.dma_start(w_raw[h][:], ws_rows[:, 2 * h : 2 * h + 2, :])

        def load_s(b):
            nc.sync.dma_start(s_rows[b][:], second[b * P : (b + 1) * P, :])

        def load_f(b):
            nc.sync.dma_start(f_rows[b][:], first[b * P : (b + 1) * P, :])

        load_s(0)
        nc.sync.dma_start(slots[:], offs)
        load_s(1)
        load_w(0)
        load_w(1)
        load_s(2)
        load_s(3)
        nc.sync.dma_start(bias_cols[:], bias.rearrange("(p t) one -> p (t one)", t=PACK))
        nc.sync.dma_start(places[:], offs2)
        for b in range(BLOCKS):
            load_f(b)

        mw = J // PACK

        def round_ws(copy, h, ms, ts):
            copy(
                w_bf[:, ts, ms, 2 * h : 2 * h + 2].rearrange("p t m r -> p m r t"),
                w_raw[h][:].rearrange("p r (m t) -> p m r t", t=PACK)[:, ms, :, ts],
            )

        def quantize_ws(ts):
            cols = slice(ts.start * P, ts.stop * P)
            nc.vector.quantize_mx(
                out=w_codes[:, cols].bitcast(FP8X4),
                scales=w_scales[:, cols],
                in_=w_bf[:, ts, :, :].rearrange("p t m r -> p (t m r)"),
            )

        def gather_second(b):
            picked = rows.tile([P, I], BF16, name="picked%d" % b, offset=picked_at[b], align_bytes=64)
            cut = S_SCALAR[b]
            if cut > 0:
                nc.scalar.activation(picked[:, : cut * 16], s_rows[b][:].indirect(slots[:, :cut]), ACT.Copy)
            if cut < I // 16:
                nc.vector.tensor_copy(picked[:, cut * 16 :], s_rows[b][:].indirect(slots[:, cut:]))
            words = picked[:].bitcast(F32)
            turned = psum.tile([P, 2, P], F32, name="turned%d" % b, offset=turned_bank[b] * BANK)
            for u in range(2):
                nc.tensor.transpose(turned[:, u, :], words[:, u : I // 2 : 2], ident[:])
            return turned

        def copy_turned(b, turned, copy):
            vt_bf = vt_bfs[b]
            copy(vt_bf.bitcast(F32).rearrange("p (e u) -> p e u", u=2), turned[:].rearrange("p u e -> p e u"))

        def quantize_vt(b, vt_bf, n):
            codes = rows.tile([P, n], U32, name="vt_codes%d" % b, offset=codes_at[b], align_bytes=64)
            scales = keep.tile([P, n], U8, name="vt_scales%d" % b, align_bytes=64)
            nc.vector.quantize_mx(out=codes[:].bitcast(FP8X4), scales=scales[:], in_=vt_bf)
            return codes, scales

        def mix(b, codes, scales, n, k=0, e0=0):
            per_bank = BANK // (4 * n)
            acc = psum.tile([P, per_bank, n], F32, name="acc%d_%d" % (b, k), offset=(acc_bank[b] + k) * BANK)
            for once in range(1):
                for s in range(per_bank):
                    t = k * per_bank + s
                    cols = slice(t * P, (t + 1) * P)
                    nc.tensor.matmul_mx(
                        out=acc[:, s, :],
                        lhsT=w_codes[:, cols].bitcast(FP8X4),
                        lhsT_scale=w_scales[:, cols],
                        rhs=codes[:, e0 : e0 + n].bitcast(FP8X4),
                        rhs_scale=scales[:, e0 : e0 + n],
                        start=True,
                        stop=True,
                    )
            return acc

        def add_bias(vb, acc, t_from, on_vector):
            count, n = acc.shape[1], acc.shape[2]
            if on_vector:
                spread = bias_cols[:, t_from : t_from + count].unsqueeze(2).to_broadcast([P, count, n])
                nc.vector.tensor_tensor(vb[:, t_from : t_from + count, :], acc[:], spread, ALU.add)
            else:
                for s in range(count):
                    t = t_from + s
                    nc.scalar.activation(vb[:, t, :], acc[:, s, :], ACT.Identity, bias=bias_cols[:, t : t + 1])

        def vb_tile(b, n):
            return rows.tile([P, PACK, n], F32, name="vb%d" % b, offset=vb_at[b], align_bytes=64)

        def gather_first(b):
            u_cols = rows.tile([P, J], F32, name="u_cols%d" % b, offset=u_at[b], align_bytes=64)
            cut = F_SCALAR[b]
            if cut == 0:
                dealt = u_cols[:].bitcast(U32).rearrange("p (t m) -> p m t", t=PACK)
                nc.vector.tensor_copy(dealt, f_rows[b][:].bitcast(U32).indirect(places[:]))
                return [u_cols[:, t * P : (t + 1) * P] for t in range(PACK)]
            nc.scalar.activation(u_cols[:, : cut * 16], f_rows[b][:].indirect(places[:, :cut]), ACT.Copy)
            if cut < J // 16:
                nc.vector.tensor_copy(u_cols[:, cut * 16 :], f_rows[b][:].indirect(places[:, cut:]))
            return [u_cols[:, t:J:PACK] for t in range(PACK)]

        def gather_part(c_from, c_to):
            dealt = u_first[:, :J].bitcast(U32).rearrange("p (t m) -> p m t", t=PACK)
            window = f_rows[0][:].bitcast(U32).indirect(places[:, c_from:c_to])
            nc.vector.tensor_copy(dealt[:, c_from * 4 : c_to * 4, :], window)

        def gather_first_dealt(b):
            u_cols = rows.tile([P, J], F32, name="u_cols%d" % b, offset=u_at[b], align_bytes=64)
            cut = J // 16 - F_SCALAR[b]
            plain = rows.tile([P, F_SCALAR[b] * 16], F32, name="u_plain%d" % b, offset=plain_at[b], align_bytes=64)
            dealt = u_cols[:].bitcast(U32).rearrange("p (t m) -> p m t", t=PACK)
            nc.scalar.activation(plain[:], f_rows[b][:].indirect(places[:, cut:]), ACT.Copy)
            nc.vector.tensor_copy(dealt[:, : cut * 4, :], f_rows[b][:].bitcast(U32).indirect(places[:, :cut]))
            return u_cols, plain, cut

        def deal_rest(u_cols, plain, cut):
            nc.vector.tensor_copy(
                u_cols[:].rearrange("p (t c i) -> p c t i", t=PACK, i=4)[:, cut:, :, :],
                plain[:].rearrange("p (c i t) -> p c t i", t=PACK, i=4),
            )
            return [u_cols[:, t * P : (t + 1) * P] for t in range(PACK)]

        def turn_first(b, columns):
            uts = []
            for bank, ts in ut_bank[b]:
                ut = psum.tile([P, len(ts), P], F32, name="ut%d_%d" % (b, bank), offset=bank * BANK)
                uts.append((ut, slice(ts.start, ts.stop)))
                for t in ts:
                    nc.tensor.transpose(ut[:, t - ts.start, :], columns[t], ident[:])
            return uts

        ys = [keep.tile([P, PACK, P], F32, name="y%d" % b) for b in range(BLOCKS)]
        out_rows = out_0.rearrange("(p t) e -> p t e", t=PACK)
        word_rows = out_1.rearrange("z p c r -> p (z c r)").bitcast(I32)

        def gate(b, uts, vb):
            for ut, ts in uts:
                e0 = P if b == 1 else 0
                nc.vector.tensor_tensor(ys[b][:, ts, :], ut[:], vb[:, ts, e0 : e0 + P], ALU.mult)
            nc.sync.dma_start(out_rows[:, :, b * P : (b + 1) * P], ys[b][:])

        def round_y(b, cols, engine):
            c0 = (b * P + cols.start) * PACK
            dst = y_bf[:, c0 : c0 + (cols.stop - cols.start) * PACK].rearrange("p (c i t) -> p c t i", i=4, t=PACK)
            src = ys[b][:, :, cols].rearrange("p t (c i) -> p c t i", i=4)
            if engine == "gpsimd":
                words = y_bf[:, c0 : c0 + P * PACK].rearrange("p (c t) -> p c t", t=PACK)
                nc.gpsimd.tensor_scalar(words, ys[b][:].rearrange("p t c -> p c t"), 1.0, -0.0, ALU.mult, ALU.add)
            elif engine == "vector":
                nc.vector.tensor_copy(dst, src)
            else:
                nc.scalar.copy(dst, src)

        def planes(b_from, b_to):
            cols = slice(b_from * P, b_to * P)
            nc.vector.quantize_mx(
                out=y_codes[:, cols].bitcast(FP8X4),
                scales=y_scales[:, cols],
                in_=y_bf[:, b_from * P * PACK : b_to * P * PACK],
            )

        def store_words(e_from, e_to):
            nc.sync.dma_start(word_rows[:, e_from:e_to], y_codes[:, e_from:e_to].bitcast(I32))

        t0 = gather_second(0)
        t1 = gather_second(1)
        low, high, every = slice(0, 2), slice(2, PACK), slice(0, PACK)
        copy_turned(0, t0, nc.scalar.copy)
        round_ws(nc.scalar.copy, 0, slice(0, W_SCALAR[0]), every)
        round_ws(nc.vector.tensor_copy, 0, slice(W_SCALAR[0], mw), every)
        copy_turned(1, t1, nc.scalar.copy)
        round_ws(nc.vector.tensor_copy, 1, slice(0, mw), low)
        round_ws(nc.vector.tensor_copy, 1, slice(W_SCALAR[1], mw), high)
        round_ws(nc.scalar.copy, 1, slice(0, W_SCALAR[1]), high)
        q01 = quantize_vt(0, vt_pair[:], 2 * P)
        quantize_ws(low)
        quantize_ws(high)
        a01 = [mix(0, *q01, 2 * P, k) for k in range(2)]
        t2 = gather_second(2)
        t3 = gather_second(3)
        vb01 = vb_tile(0, 2 * P)
        add_bias(vb01, a01[0], 0, True)
        add_bias(vb01, a01[1], 2, False)
        copy_turned(2, t2, nc.scalar.copy)
        copy_turned(3, t3, nc.scalar.copy)
        gather_part(0, F_EARLY)
        a23 = [mix(2, *quantize_vt(2, vt_bfs[2], P), P)]
        gather_part(F_EARLY, J // 16)
        a23.append(mix(3, *quantize_vt(3, vt_bfs[3], P), P))
        u0 = turn_first(0, [u_first[:, t * P : (t + 1) * P] for t in range(PACK)])
        u1 = turn_first(1, gather_first(1))
        whole = slice(0, P)
        halves = (slice(0, 64), slice(64, P))
        vb2 = vb_tile(2, P)
        vb3 = vb_tile(3, P)
        add_bias(vb2, a23[0], 0, False)
        u2 = turn_first(2, deal_rest(*gather_first_dealt(2)))
        u3 = turn_first(3, gather_first(3))
        add_bias(vb3, a23[1], 0, False)
        gate(0, u0, vb01)
        round_y(0, whole, "gpsimd")
        gate(1, u1, vb01)
        round_y(1, whole, "gpsimd")
        gate(2, u2, vb2)
        round_y(2, whole, "scalar")
        gate(3, u3, vb3)
        round_y(3, halves[0], "scalar")
        planes(0, 2)
        round_y(3, halves[1], "vector")
        planes(2, 3)
        planes(3, 4)
        store_words(0, 4 * P)

        scale_rows = out_2.rearrange("z q c -> (z q) c").bitcast(I32)
        for quad in range(4):
            queue = nc.scalar
            queue.dma_start(
                scale_rows[4 * quad : 4 * quad + 4, :], y_scales[32 * quad : 32 * quad + 4, :].bitcast(I32)
            )
